import numpy as np
import ml_dtypes


def mxq(x, axis, fmt="e4m3"):
    dtype, down = {"e4m3": (ml_dtypes.float8_e4m3fn, 7), "e5m2": (ml_dtypes.float8_e5m2, 14)}[fmt]
    v = np.moveaxis(np.asarray(x, np.float32).astype(ml_dtypes.bfloat16).astype(np.float64), axis, -1)
    blocks = v.reshape(v.shape[:-1] + (-1, 32))
    amax = np.abs(blocks).max(-1, keepdims=True)
    byte = np.maximum(np.where(amax > 0, np.frexp(amax)[1] - 1 + 127, 0) - down, 1)
    scale = np.exp2(byte - 127.0)
    codes = (blocks / scale).astype(np.float32).astype(dtype).astype(np.float64)
    return np.moveaxis((codes * scale).reshape(v.shape), -1, axis)


WIDE = False


def mx_kscale(k):
    if not WIDE:
        return np.ones(k)
    levels = np.array([24, -24, 12, -12, 0])
    if k % 512:
        return np.exp2(np.random.permutation(np.resize(levels, k // 32))).repeat(32)
    a = np.empty((k // 512, 16))
    for p in range(k // 512):
        a[p, :8] = np.random.permutation(np.resize(levels, 8))
        for g in range(8):
            far = levels[np.abs(levels - a[p, g]) >= 10]
            a[p, g + 8] = far[np.random.randint(len(far))]
    return np.exp2(a.ravel()).repeat(32)


def f64(x):
    return np.asarray(x).astype(np.float64)


def striped(idx):
    return np.tile(idx.reshape(-1, 16).T, (8, 1)).astype(np.uint16)


def unstriped(offs):
    return offs[:16].T.reshape(-1).astype(np.int64)


E2M1 = np.array([0.0, 0.5, 1.0, 1.5, 2.0, 3.0, 4.0, 6.0, -0.0, -0.5, -1.0, -1.5, -2.0, -3.0, -4.0, -6.0])


def pack_weight(w, fmt):
    k, n = w.shape
    w = f64(np.asarray(w, np.float32).astype(ml_dtypes.bfloat16)).reshape(k // 32, 32, n)
    amax = np.abs(w).max(1)
    if fmt == "e4m3":
        byte = np.frexp(amax)[1] - 1 + 127 - 7
    else:
        mant, ex = np.frexp(amax / 6.0)
        byte = np.where(mant > 0.5, ex, ex - 1) + 127
    byte = np.clip(np.where(amax > 0, byte, 1), 1, 254)
    scaled = (w * np.exp2(127.0 - byte)[:, None, :]).reshape(k, n).astype(np.float32)
    by_word = np.ascontiguousarray(scaled.reshape(k // 512, 128, 4, n).transpose(0, 1, 3, 2))
    if fmt == "e4m3":
        words = by_word.astype(ml_dtypes.float8_e4m3fn).view(np.uint8)
    else:
        c = by_word.astype(ml_dtypes.float4_e2m1fn).view(np.uint8) & 0xF
        words = (c[..., 0::2] | (c[..., 1::2] << 4)).reshape(k // 512, 128, 2 * n)
    return np.ascontiguousarray(words), np.ascontiguousarray(byte.astype(np.uint8).reshape(k // 512, 16, n))


def unpack_weight(words, scales, fmt):
    g, _, n = scales.shape
    words = np.ascontiguousarray(words).reshape(g, 128, n, -1)
    if fmt == "e4m3":
        vals = words.view(ml_dtypes.float8_e4m3fn).astype(np.float64)
    else:
        nib = np.empty((g, 128, n, 4), np.uint8)
        nib[..., 0::2] = words & 0xF
        nib[..., 1::2] = words >> 4
        vals = E2M1[nib]
    vals = vals * np.repeat(np.exp2(scales.astype(np.float64) - 127.0), 8, axis=1)[..., None]
    return vals.transpose(0, 1, 3, 2).reshape(g * 512, n)


def pack_table4(v):
    words, scales = pack_weight(v, "e2m1")
    g, t = words.shape[0] // 2, v.shape[1]
    return np.ascontiguousarray(words.reshape(g, 2, 128, t, 2).transpose(0, 2, 3, 1, 4).reshape(g, 128, t, 4)), scales


def unpack_table4(words, scales):
    g, _, t, _ = words.shape
    return unpack_weight(words.reshape(g, 128, t, 2, 2).transpose(0, 3, 1, 2, 4).reshape(2 * g, 128, 2 * t), scales, "e2m1")


K, F, N, T, J = 1024, 1024, 256, 4096, 2048


def setup_inputs():
    n = np.random.standard_normal
    s = mx_kscale(K)[:, None]
    u = mx_kscale(F)[:, None]
    p_tab = pack_table4(n((K, T)) * s)
    p_co = pack_weight(n((K, F)) / np.sqrt(K) / s, "e2m1")
    p_si = pack_weight(n((K, F)) / np.sqrt(K) / s, "e2m1")
    return {
        "tab_words": p_tab[0],
        "tab_scales": p_tab[1],
        "co_words": p_co[0],
        "co_scales": p_co[1],
        "si_words": p_si[0],
        "si_scales": p_si[1],
        "gn": (np.random.uniform(0.5, 2.0, F) * u[:, 0]).astype(np.float32),
        "fb": (np.abs(n((F, N))) / F / u).astype(np.float32),
        "offs": striped(np.random.permutation(T)[:J]),
    }


def reference(tab_words, tab_scales, co_words, co_scales, si_words, si_scales, gn, fb, offs):
    idx = unstriped(offs)
    tab_ = unpack_table4(tab_words, tab_scales)[:, idx]
    co_ = unpack_weight(co_words, co_scales, "e2m1")
    si_ = unpack_weight(si_words, si_scales, "e2m1")
    re = co_.T @ tab_
    im = si_.T @ tab_
    h = f64(gn)[:, None] * ((re) ** 2 + (im) ** 2)
    h_ = mxq(h, 0, "e4m3")
    fb_ = mxq(f64(fb), 0, "e4m3")
    y = fb_.T @ h_
    return np.log(y + 1.0)

@@ -1,0 +1,295 @@
+from contextlib import ExitStack
+
+import concourse.mybir as mybir
+from concourse.masks import make_identity
+
+K, F, N, T, J = 1024, 1024, 256, 4096, 2048
+FLOPS = 2 * (2 * K * F * J + F * N * J)
+
+F32 = mybir.dt.float32
+BF16 = mybir.dt.bfloat16
+I32 = mybir.dt.int32
+U32 = mybir.dt.uint32
+U16 = mybir.dt.uint16
+U8 = mybir.dt.uint8
+FP4X4 = mybir.dt.float4_e2m1fn_x4
+FP8X4 = mybir.dt.float8_e4m3fn_x4
+ALU = mybir.AluOpType
+ACT = mybir.ActivationFunctionType
+
+P = 128
+CHUNK = 512
+CHUNKS = J // CHUNK
+WIDTHS = (384, 640)
+TAB_AT = ((0, 0), (1, 256), (1, 384), (1, 512))
+W_AT = (((0, 128), (1, 0)), ((0, 256), (1, 128)))
+ON_VECTOR = ()
+SQRT_FLOOR = 2.0 ** -100
+
+
+def tile_list_meltab_log_kernel(
+    tc, tab_words, tab_scales, co_words, co_scales, si_words, si_scales, gn, fb, offs, out
+):
+    nc = tc.nc
+    with ExitStack() as ctx:
+        keep = ctx.enter_context(tc.tile_pool(name="keep", bufs=1))
+        sq_pool = ctx.enter_context(tc.tile_pool(name="sq", bufs=3))
+        h_pool = ctx.enter_context(tc.tile_pool(name="h", bufs=2))
+        hq_pool = ctx.enter_context(tc.tile_pool(name="hq", bufs=6))
+        y_pool = ctx.enter_context(tc.tile_pool(name="y", bufs=4))
+        psum = ctx.enter_context(tc.psum_pool(name="psum", bufs=8))
+
+        offsets = keep.tile([P, J // 16], U16, name="offsets")
+        tab_win = keep.tile([P, T], I32, name="tab_win", align_bytes=64)
+        sc_win = keep.tile([P, T // 4], I32, name="sc_win", align_bytes=64)
+        wsc_raw = keep.tile([32, 2, F // 4], I32, name="wsc_raw", align_bytes=64)
+        staged = [keep.tile([32, WIDTHS[s]], I32, name="staged%d" % s, align_bytes=64) for s in range(2)]
+        w_raw0 = keep.tile([P, 2, 2, 256], I32, name="w_raw0", align_bytes=64)
+        planes = [keep.tile([P, 2, WIDTHS[s]], I32, name="planes%d" % s, align_bytes=64) for s in range(2)]
+        parted = keep.tile([P, CHUNKS, 2, CHUNK], U16, name="parted", align_bytes=64)
+        w_codes = keep.tile([P, 2, 2, 4, 2, 64], I32, name="w_codes", align_bytes=64)
+        gn_rows = keep.tile([P, 2, P], F32, name="gn_rows")
+        ident = keep.tile([P, P], F32, name="ident")
+
+        nc.gpsimd.memset(gn_rows[:], 0.0)
+        nc.vector.memset(sc_win[32:64, :], 0)
+        nc.vector.memset(sc_win[64:128, :], 0)
+        nc.vector.memset(planes[0][:], 0)
+        nc.vector.memset(planes[1][:], 0)
+
+        nc.scalar.dma_start(out=sc_win[0:32, :], in_=tab_scales.rearrange("a q t -> (a q) t").bitcast(I32))
+        nc.sync.dma_start(offsets[:], offs)
+        words_in = (co_words, si_words)
+        scales_in = (co_scales, si_scales)
+
+        def load_words(queue, raw, b):
+            for m in range(2):
+                src = words_in[m][:, :, 1024 * b : 1024 * (b + 1)].rearrange("a p x -> p a x").bitcast(I32)
+                queue.dma_start(out=raw[:, m, :, :], in_=src)
+
+        for m in range(2):
+            nc.scalar.dma_start(out=wsc_raw[:, m, :], in_=scales_in[m].rearrange("a q x -> (a q) x").bitcast(I32))
+        load_words(nc.scalar, w_raw0, 0)
+        nc.sync.dma_start(
+            out=gn_rows[0:4, :, :].rearrange("t b (q e) -> t (b q) e", e=4),
+            in_=gn.rearrange("(bq t e) -> t bq e", t=4, e=4),
+        )
+        nc.scalar.dma_start(out=tab_win[:], in_=tab_words[0].rearrange("p t x -> p (t x)").bitcast(I32), max_dma_last_dim=4096)
+        make_identity(nc, ident[:])
+
+        def gather_scales(c, sc_got, i):
+            nc.vector.tensor_copy(
+                out=sc_got[:].bitcast(U8)[:, CHUNK * i : CHUNK * (i + 1)],
+                in_=sc_win[:].bitcast(U8).indirect(offsets[:, 32 * c : 32 * (c + 1)]),
+            )
+
+        def move_scales(s):
+            for a in range(2):
+                for q in range(4):
+                    nc.sync.dma_start(
+                        out=planes[s][32 * q : 32 * q + 4, a, :],
+                        in_=staged[s][16 * a + 4 * q : 16 * a + 4 * q + 4, :],
+                    )
+
+        def stage_scales(c0, c1, sc_got):
+            s, lo = TAB_AT[c0]
+            nc.vector.tensor_copy(out=staged[s][:, lo : lo + 128 * (c1 - c0)], in_=sc_got[0:32, :])
+
+        def gather_words(c, got):
+            nc.vector.tensor_copy(
+                out=got[:].bitcast(U32), in_=tab_win[:].bitcast(U32).indirect(offsets[:, 32 * c : 32 * (c + 1)])
+            )
+            halves = got[:].bitcast(U16).rearrange("p (j d) -> p d j", d=2)
+            if c == 0:
+                for d in range(2):
+                    nc.vector.tensor_copy(out=parted[:, c, d, :], in_=halves[:, d, :])
+            else:
+                nc.vector.tensor_copy(out=parted[:, c, :, :], in_=halves)
+
+        def order_words(raw, m, b):
+            nc.vector.tensor_copy(
+                out=w_codes[:, m, b].rearrange("p t a (q w) -> p t (a q) w", w=2),
+                in_=raw[:, m].rearrange("p a (q t w) -> p t (a q) w", t=4, w=2),
+            )
+
+        def order_scales(m, b):
+            s, lo = W_AT[m][b]
+            nc.vector.tensor_copy(
+                out=staged[s][:, lo : lo + 128].rearrange("p (t q) -> p t q", t=4),
+                in_=wsc_raw[:, m, 128 * b : 128 * (b + 1)].rearrange("p (q t) -> p t q", t=4),
+            )
+
+        sc_first = keep.tile([P, 128], I32, name="sc_first", tag="reused", align_bytes=64)
+        gather_scales(0, sc_first, 0)
+        order_scales(0, 0)
+        order_scales(1, 0)
+        stage_scales(0, 1, sc_first)
+        move_scales(0)
+        order_words(w_raw0, 0, 0)
+        order_words(w_raw0, 1, 0)
+
+        gain_ps = psum.tile([P, 512], F32, name="bank")
+        for b in range(2):
+            nc.tensor.transpose(gain_ps[:, P * b : P * (b + 1)], gn_rows[:, b, :], ident[:])
+        gain = gain_ps[:, 0 : 2 * P].rearrange("p (b x) -> p b x", b=2)[:, :, 0:4]
+        mag = keep.tile([P, 2, 4], F32, name="mag")
+        nc.scalar.activation(out=mag[:], in_=gain, func=ACT.Abs)
+        mag8 = mag[:].rearrange("p b t -> p (b t)")
+        inv_root = keep.tile([P, 8], F32, name="inv_root")
+        nc.scalar.activation(out=inv_root[:], in_=mag8, func=ACT.Abs_reciprocal_sqrt, bias=SQRT_FLOOR)
+        sign = keep.tile([P, 2, 4], F32, name="sign")
+        nc.scalar.activation(out=sign[:], in_=gain, func=ACT.Sign)
+        warm = keep.tile([P, 1], F32, name="warm")
+        nc.scalar.activation(out=warm[:], in_=inv_root[:, 0:1], func=ACT.Ln)
+        root0 = keep.tile([P, 8], F32, name="root0")
+        nc.gpsimd.tensor_tensor(out=root0[:], in0=mag8, in1=inv_root[:], op=ALU.mult)
+        near_one = keep.tile([P, 8], F32, name="near_one")
+        nc.gpsimd.tensor_tensor(out=near_one[:], in0=root0[:], in1=inv_root[:], op=ALU.mult)
+        mend = keep.tile([P, 8], F32, name="mend")
+        nc.gpsimd.tensor_scalar(out=mend[:], in0=near_one[:], scalar1=-0.5, scalar2=1.5, op0=ALU.mult, op1=ALU.add)
+        root = keep.tile([P, 8], F32, name="root")
+        nc.gpsimd.tensor_tensor(out=root[:], in0=root0[:], in1=mend[:], op=ALU.mult)
+
+        got0 = keep.tile([P, CHUNK], I32, name="got0", tag="got", align_bytes=64)
+        gather_words(0, got0)
+
+        sc_rest = keep.tile([P, 128 * (CHUNKS - 1)], I32, name="sc_rest", tag="reused", align_bytes=64)
+        for c in range(1, CHUNKS):
+            gather_scales(c, sc_rest, c - 1)
+        order_scales(0, 1)
+        order_scales(1, 1)
+        stage_scales(1, CHUNKS, sc_rest)
+        w_raw1 = keep.tile([P, 2, 2, 256], I32, name="w_raw1", tag="reused", align_bytes=64)
+        load_words(nc.sync, w_raw1, 1)
+        move_scales(1)
+
+        def power(j0, width, b, order):
+            c, o = j0 // CHUNK, j0 % CHUNK
+            ts, tlo = TAB_AT[c]
+            sq = sq_pool.tile([P, 4, 2, width], F32, name="sq")
+            bank = None
+            for t, m in order:
+                if width == CHUNK or m == 0:
+                    bank = psum.tile([P, 512], F32, name="bank")
+                lo = 0 if width == CHUNK else m * width
+                ws, wlo = W_AT[m][b]
+                for a in range(2):
+                    nc.tensor.matmul_mx(
+                        out=bank[:, lo : lo + width],
+                        lhsT=w_codes[:, m, b, t, a, :].bitcast(U8).bitcast(FP4X4),
+                        lhsT_scale=planes[ws][:, a, wlo + 32 * t : wlo + 32 * (t + 1)].bitcast(U8),
+                        rhs=parted[:, c, a, o : o + width].bitcast(U8).bitcast(FP4X4),
+                        rhs_scale=planes[ts][:, a, tlo + o // 4 : tlo + (o + width) // 4].bitcast(U8),
+                        start=(a == 0),
+                        stop=(a == 1),
+                    )
+                scale = root[:, 4 * b + t : 4 * b + t + 1]
+                if width == CHUNK and m == 0 and (2 * c + b, t) in ON_VECTOR:
+                    scaled = y_pool.tile([P, 512], F32, name="scaled")
+                    nc.vector.tensor_scalar(out=scaled[:], in0=bank[:], scalar1=scale, scalar2=None, op0=ALU.mult)
+                    nc.vector.tensor_tensor(out=sq[:, t, m, :], in0=scaled[:], in1=scaled[:], op=ALU.mult)
+                elif width == CHUNK:
+                    nc.scalar.activation(out=sq[:, t, m, :], in_=bank[:], func=ACT.Square, scale=scale)
+                elif m == 1:
+                    nc.scalar.activation(
+                        out=sq[:, t].rearrange("p m w -> p (m w)"), in_=bank[:, 0 : 2 * width], func=ACT.Square, scale=scale
+                    )
+            h = h_pool.tile([P, width, 4], BF16, name="h", align_bytes=64)
+            codes = hq_pool.tile([P, width], U32, name="codes", align_bytes=64)
+            plane = hq_pool.tile([P, width], U8, name="plane", align_bytes=64)
+            half = width // 2
+            for u in range(2):
+                cols = slice(half * u, half * (u + 1))
+                nc.vector.tensor_tensor(
+                    out=h[:, cols, :].rearrange("p (c i) t -> p c t i", i=4),
+                    in0=sq[:, :, 0, cols].rearrange("p t (c i) -> p c t i", i=4),
+                    in1=sq[:, :, 1, cols].rearrange("p t (c i) -> p c t i", i=4),
+                    op=ALU.add,
+                )
+            for u in range(2):
+                cols = slice(half * u, half * (u + 1))
+                nc.vector.quantize_mx(
+                    out=codes[:, cols].bitcast(FP8X4),
+                    scales=plane[:, cols],
+                    in_=h[:, cols, :].rearrange("p j t -> p (j t)"),
+                )
+            return codes, plane
+
+        fb_codes = keep.tile([P, 2, N], U32, name="fb_codes", align_bytes=64)
+        fb_plane = keep.tile([P, 2, N], U8, name="fb_plane", align_bytes=64)
+
+        def prepare_fb():
+            fb_raw = keep.tile([P, 2, 4, N], F32, name="fb_raw", tag="reused", align_bytes=64)
+            rows = fb.rearrange("(b q t e) n -> b e q t n", b=2, t=4, e=4)
+            for b in range(2):
+                for e in range(4):
+                    nc.sync.dma_start(out=fb_raw[e:P:4, b, :, :], in_=rows[b, e])
+            fb_bf = h_pool.tile([P, 2, N, 4], BF16, name="h", align_bytes=64)
+            for b in range(2):
+                nc.vector.tensor_tensor(
+                    out=fb_bf[:, b].rearrange("p (c i) t -> p c t i", i=4),
+                    in0=fb_raw[:, b].rearrange("p t (c i) -> p c t i", i=4),
+                    in1=sign[:, b, :].unsqueeze(1).unsqueeze(3).to_broadcast([P, N // 4, 4, 4]),
+                    op=ALU.mult,
+                )
+            nc.vector.quantize_mx(
+                out=fb_codes[:].rearrange("p b n -> p (b n)").bitcast(FP8X4),
+                scales=fb_plane[:].rearrange("p b n -> p (b n)"),
+                in_=fb_bf[:].rearrange("p b n t -> p (b n t)"),
+            )
+
+        def filters(j0, width, halves):
+            bank = None
+            for i in range(2):
+                if width == CHUNK or i == 0:
+                    bank = psum.tile([P, 512], F32, name="bank")
+                lo = 0 if width == CHUNK else i * width
+                for b in range(2):
+                    codes, plane, o = halves[b]
+                    nc.tensor.matmul_mx(
+                        out=bank[:, lo : lo + width],
+                        lhsT=fb_codes[:, b, P * i : P * (i + 1)].bitcast(FP8X4),
+                        lhsT_scale=fb_plane[:, b, P * i : P * (i + 1)],
+                        rhs=codes[:, o : o + width].bitcast(FP8X4),
+                        rhs_scale=plane[:, o : o + width],
+                        start=(b == 0),
+                        stop=(b == 1),
+                    )
+                if width == CHUNK:
+                    y = y_pool.tile([P, 512], F32, name="y")
+                    nc.scalar.activation(out=y[:], in_=bank[:], func=ACT.Ln, bias=1.0)
+                    nc.sync.dma_start(out=out[P * i : P * (i + 1), j0 : j0 + width], in_=y[:])
+                elif i == 1:
+                    y = y_pool.tile([P, 512], F32, name="y")
+                    nc.scalar.activation(out=y[:, 0 : 2 * width], in_=bank[:, 0 : 2 * width], func=ACT.Ln, bias=1.0)
+                    nc.sync.dma_start(
+                        out=out[:, j0 : j0 + width].rearrange("(i p) w -> p i w", p=P),
+                        in_=y[:, 0 : 2 * width].rearrange("p (i w) -> p i w", i=2),
+                    )
+
+        by_t = [(t, m) for t in range(4) for m in range(2)]
+        waiting = None
+        for c in range(CHUNKS):
+            j0 = CHUNK * c
+            low = power(j0, CHUNK, 0, by_t)
+            if c == 0:
+                order_words(w_raw1, 0, 1)
+                order_words(w_raw1, 1, 1)
+            if waiting is not None and c > 1:
+                filters(*waiting)
+            if c + 1 < CHUNKS:
+                got = keep.tile([P, CHUNK], I32, name="got%d" % (c + 1), tag="got", align_bytes=64)
+                gather_words(c + 1, got)
+                high = power(j0, CHUNK, 1, by_t)
+                if c == 1:
+                    filters(*waiting)
+                waiting = (j0, CHUNK, ((low[0], low[1], 0), (high[0], high[1], 0)))
+            else:
+                pieces = []
+                for o, width in ((0, 256), (256, 128), (384, 128)):
+                    high = power(j0 + o, width, 1, by_t)
+                    pieces.append((j0 + o, width, ((low[0], low[1], o), (high[0], high[1], 0))))
+                for piece in pieces:
+                    filters(*piece)
+            if c == 0:
+                prepare_fb()

@@ -23,7 +23,7 @@ CHUNKS = J // CHUNK
 WIDTHS = (384, 640)
 TAB_AT = ((0, 0), (1, 256), (1, 384), (1, 512))
 W_AT = (((0, 128), (1, 0)), ((0, 256), (1, 128)))
-ON_VECTOR = ()
+ON_VECTOR = ((3, 3), (4, 3), (5, 3), (6, 3))
 SQRT_FLOOR = 2.0 ** -100
 
 
@@ -139,8 +139,6 @@ def tile_list_meltab_log_kernel(
         nc.scalar.activation(out=inv_root[:], in_=mag8, func=ACT.Abs_reciprocal_sqrt, bias=SQRT_FLOOR)
         sign = keep.tile([P, 2, 4], F32, name="sign")
         nc.scalar.activation(out=sign[:], in_=gain, func=ACT.Sign)
-        warm = keep.tile([P, 1], F32, name="warm")
-        nc.scalar.activation(out=warm[:], in_=inv_root[:, 0:1], func=ACT.Ln)
         root0 = keep.tile([P, 8], F32, name="root0")
         nc.gpsimd.tensor_tensor(out=root0[:], in0=mag8, in1=inv_root[:], op=ALU.mult)
         near_one = keep.tile([P, 8], F32, name="near_one")

@@ -139,6 +139,8 @@ def tile_list_meltab_log_kernel(
         nc.scalar.activation(out=inv_root[:], in_=mag8, func=ACT.Abs_reciprocal_sqrt, bias=SQRT_FLOOR)
         sign = keep.tile([P, 2, 4], F32, name="sign")
         nc.scalar.activation(out=sign[:], in_=gain, func=ACT.Sign)
+        warm = keep.tile([P, 1], F32, name="warm")
+        nc.scalar.activation(out=warm[:], in_=inv_root[:, 0:1], func=ACT.Ln)
         root0 = keep.tile([P, 8], F32, name="root0")
         nc.gpsimd.tensor_tensor(out=root0[:], in0=mag8, in1=inv_root[:], op=ALU.mult)
         near_one = keep.tile([P, 8], F32, name="near_one")
@@ -154,6 +156,18 @@ def tile_list_meltab_log_kernel(
         sc_rest = keep.tile([P, 128 * (CHUNKS - 1)], I32, name="sc_rest", tag="reused", align_bytes=64)
         for c in range(1, CHUNKS):
             gather_scales(c, sc_rest, c - 1)
+        warm_bank = psum.tile([P, 512], F32, name="bank")
+        raw_codes = w_raw0[:, 0, 0, :]
+        for scales in (sc_rest[:, 256:384], sc_win[:, 0:128], sc_win[:, 0:128], sc_win[:, 0:128]):
+            nc.tensor.matmul_mx(
+                out=warm_bank[:],
+                lhsT=raw_codes[:, 0:64].bitcast(U8).bitcast(FP4X4),
+                lhsT_scale=scales[:, 0:32].bitcast(U8),
+                rhs=raw_codes.bitcast(U8).bitcast(FP4X4),
+                rhs_scale=scales.bitcast(U8),
+                start=True,
+                stop=True,
+            )
         order_scales(0, 1)
         order_scales(1, 1)
         stage_scales(1, CHUNKS, sc_rest)

@@ -20,10 +20,10 @@ ACT = mybir.ActivationFunctionType
 P = 128
 CHUNK = 512
 CHUNKS = J // CHUNK
-WIDTHS = (384, 640)
-TAB_AT = ((0, 0), (1, 256), (1, 384), (1, 512))
-W_AT = (((0, 128), (1, 0)), ((0, 256), (1, 128)))
-ON_VECTOR = ((3, 3), (4, 3), (5, 3), (6, 3))
+WIDTHS = (384, 384, 256)
+TAB_AT = ((0, 0), (1, 0), (2, 0), (2, 128))
+W_AT = (((0, 128), (1, 128)), ((0, 256), (1, 256)))
+ON_VECTOR = ((2, 3), (3, 3), (4, 3), (5, 3), (6, 3))
 SQRT_FLOOR = 2.0 ** -100
 
 
@@ -35,41 +35,42 @@ def tile_list_meltab_log_kernel(
         keep = ctx.enter_context(tc.tile_pool(name="keep", bufs=1))
         sq_pool = ctx.enter_context(tc.tile_pool(name="sq", bufs=3))
         h_pool = ctx.enter_context(tc.tile_pool(name="h", bufs=2))
-        hq_pool = ctx.enter_context(tc.tile_pool(name="hq", bufs=6))
+        hq_pool = ctx.enter_context(tc.tile_pool(name="hq", bufs=8))
         y_pool = ctx.enter_context(tc.tile_pool(name="y", bufs=4))
         psum = ctx.enter_context(tc.psum_pool(name="psum", bufs=8))
 
         offsets = keep.tile([P, J // 16], U16, name="offsets")
         tab_win = keep.tile([P, T], I32, name="tab_win", align_bytes=64)
         sc_win = keep.tile([P, T // 4], I32, name="sc_win", align_bytes=64)
-        wsc_raw = keep.tile([32, 2, F // 4], I32, name="wsc_raw", align_bytes=64)
-        staged = [keep.tile([32, WIDTHS[s]], I32, name="staged%d" % s, align_bytes=64) for s in range(2)]
-        w_raw0 = keep.tile([P, 2, 2, 256], I32, name="w_raw0", align_bytes=64)
-        planes = [keep.tile([P, 2, WIDTHS[s]], I32, name="planes%d" % s, align_bytes=64) for s in range(2)]
-        parted = keep.tile([P, CHUNKS, 2, CHUNK], U16, name="parted", align_bytes=64)
-        w_codes = keep.tile([P, 2, 2, 4, 2, 64], I32, name="w_codes", align_bytes=64)
+        wsc_raw = keep.tile([32, 2, F // 4], I32, name="wsc_raw", tag="slot_w", align_bytes=64)
+        co_raw0 = keep.tile([P, 2, 256], I32, name="co_raw0", align_bytes=64)
+        planes = [keep.tile([P, 2 * WIDTHS[s]], I32, name="planes%d" % s, align_bytes=64) for s in range(3)]
+        parted = [
+            [keep.tile([P, CHUNK], U16, name="parted%d_%d" % (c, d), align_bytes=64) for d in range(2)] for c in range(CHUNKS)
+        ]
+        w_codes = [
+            [keep.tile([P, 4 * 2 * 64], I32, name="w_codes%d_%d" % (m, b), align_bytes=64) for b in range(2)] for m in range(2)
+        ]
         gn_rows = keep.tile([P, 2, P], F32, name="gn_rows")
         ident = keep.tile([P, P], F32, name="ident")
 
         nc.gpsimd.memset(gn_rows[:], 0.0)
-        nc.vector.memset(sc_win[32:64, :], 0)
+        nc.gpsimd.memset(sc_win[32:64, :], 0)
         nc.vector.memset(sc_win[64:128, :], 0)
-        nc.vector.memset(planes[0][:], 0)
-        nc.vector.memset(planes[1][:], 0)
+        nc.vector.memset(planes[0][:, 128:], 0)
 
         nc.scalar.dma_start(out=sc_win[0:32, :], in_=tab_scales.rearrange("a q t -> (a q) t").bitcast(I32))
         nc.sync.dma_start(offsets[:], offs)
         words_in = (co_words, si_words)
         scales_in = (co_scales, si_scales)
 
-        def load_words(queue, raw, b):
-            for m in range(2):
-                src = words_in[m][:, :, 1024 * b : 1024 * (b + 1)].rearrange("a p x -> p a x").bitcast(I32)
-                queue.dma_start(out=raw[:, m, :, :], in_=src)
+        def load_words(queue, raw, m, b):
+            src = words_in[m][:, :, 1024 * b : 1024 * (b + 1)].rearrange("a p x -> p a x").bitcast(I32)
+            queue.dma_start(out=raw, in_=src)
 
         for m in range(2):
             nc.scalar.dma_start(out=wsc_raw[:, m, :], in_=scales_in[m].rearrange("a q x -> (a q) x").bitcast(I32))
-        load_words(nc.scalar, w_raw0, 0)
+        load_words(nc.scalar, co_raw0[:], 0, 0)
         nc.sync.dma_start(
             out=gn_rows[0:4, :, :].rearrange("t b (q e) -> t (b q) e", e=4),
             in_=gn.rearrange("(bq t e) -> t bq e", t=4, e=4),
@@ -84,49 +85,51 @@ def tile_list_meltab_log_kernel(
             )
 
         def move_scales(s):
+            w = WIDTHS[s]
             for a in range(2):
                 for q in range(4):
-                    nc.sync.dma_start(
-                        out=planes[s][32 * q : 32 * q + 4, a, :],
-                        in_=staged[s][16 * a + 4 * q : 16 * a + 4 * q + 4, :],
-                    )
+                    if a or q:
+                        nc.sync.dma_start(
+                            out=planes[s][32 * q : 32 * q + 4, a * w : (a + 1) * w],
+                            in_=planes[s][16 * a + 4 * q : 16 * a + 4 * q + 4, 0:w],
+                        )
 
         def stage_scales(c0, c1, sc_got):
             s, lo = TAB_AT[c0]
-            nc.vector.tensor_copy(out=staged[s][:, lo : lo + 128 * (c1 - c0)], in_=sc_got[0:32, :])
+            nc.vector.tensor_copy(out=planes[s][:, lo : lo + 128 * (c1 - c0)], in_=sc_got[:])
 
         def gather_words(c, got):
             nc.vector.tensor_copy(
                 out=got[:].bitcast(U32), in_=tab_win[:].bitcast(U32).indirect(offsets[:, 32 * c : 32 * (c + 1)])
             )
             halves = got[:].bitcast(U16).rearrange("p (j d) -> p d j", d=2)
-            if c == 0:
-                for d in range(2):
-                    nc.vector.tensor_copy(out=parted[:, c, d, :], in_=halves[:, d, :])
-            else:
-                nc.vector.tensor_copy(out=parted[:, c, :, :], in_=halves)
+            for d in range(2):
+                nc.vector.tensor_copy(out=parted[c][d][:], in_=halves[:, d, :])
 
         def order_words(raw, m, b):
             nc.vector.tensor_copy(
-                out=w_codes[:, m, b].rearrange("p t a (q w) -> p t (a q) w", w=2),
-                in_=raw[:, m].rearrange("p a (q t w) -> p t (a q) w", t=4, w=2),
+                out=w_codes[m][b][:].rearrange("p (t x w) -> p t x w", t=4, w=2),
+                in_=raw.rearrange("p a (q t w) -> p t (a q) w", t=4, w=2),
             )
 
         def order_scales(m, b):
             s, lo = W_AT[m][b]
             nc.vector.tensor_copy(
-                out=staged[s][:, lo : lo + 128].rearrange("p (t q) -> p t q", t=4),
+                out=planes[s][0:32, lo : lo + 128].rearrange("p (t q) -> p t q", t=4),
                 in_=wsc_raw[:, m, 128 * b : 128 * (b + 1)].rearrange("p (q t) -> p t q", t=4),
             )
 
-        sc_first = keep.tile([P, 128], I32, name="sc_first", tag="reused", align_bytes=64)
+        sc_first = keep.tile([P, 128], I32, name="sc_first", tag="slot_a", align_bytes=64)
         gather_scales(0, sc_first, 0)
         order_scales(0, 0)
         order_scales(1, 0)
         stage_scales(0, 1, sc_first)
         move_scales(0)
-        order_words(w_raw0, 0, 0)
-        order_words(w_raw0, 1, 0)
+        si_raw0 = keep.tile([P, 2, 256], I32, name="si_raw0", tag="slot_a", align_bytes=64)
+        load_words(nc.sync, si_raw0[:], 1, 0)
+        order_words(co_raw0[:], 0, 0)
+        nc.vector.memset(planes[1][:, 128:], 0)
+        nc.vector.memset(planes[2][:, 256:], 0)
 
         gain_ps = psum.tile([P, 512], F32, name="bank")
         for b in range(2):
@@ -150,30 +153,38 @@ def tile_list_meltab_log_kernel(
         root = keep.tile([P, 8], F32, name="root")
         nc.gpsimd.tensor_tensor(out=root[:], in0=root0[:], in1=mend[:], op=ALU.mult)
 
-        got0 = keep.tile([P, CHUNK], I32, name="got0", tag="got", align_bytes=64)
-        gather_words(0, got0)
-
-        sc_rest = keep.tile([P, 128 * (CHUNKS - 1)], I32, name="sc_rest", tag="reused", align_bytes=64)
-        for c in range(1, CHUNKS):
-            gather_scales(c, sc_rest, c - 1)
+        sc_second = keep.tile([P, 128], I32, name="sc_second", tag="slot_s", align_bytes=64)
+        gather_scales(1, sc_second, 0)
+        order_scales(0, 1)
+        order_scales(1, 1)
+        stage_scales(1, 2, sc_second)
+        sc_third = keep.tile([P, 128], I32, name="sc_third", tag="slot_s", align_bytes=64)
+        gather_scales(2, sc_third, 0)
+        stage_scales(2, 3, sc_third)
         warm_bank = psum.tile([P, 512], F32, name="bank")
-        raw_codes = w_raw0[:, 0, 0, :]
-        for scales in (sc_rest[:, 256:384], sc_win[:, 0:128], sc_win[:, 0:128], sc_win[:, 0:128]):
+        raw_codes = co_raw0[:, 0, :]
+        for codes_in, scales in [(raw_codes, planes[1][:, 0:128])] * 2 + [(tab_win[:, 0:256], sc_win[:, 0:128])] * 3:
             nc.tensor.matmul_mx(
                 out=warm_bank[:],
                 lhsT=raw_codes[:, 0:64].bitcast(U8).bitcast(FP4X4),
                 lhsT_scale=scales[:, 0:32].bitcast(U8),
-                rhs=raw_codes.bitcast(U8).bitcast(FP4X4),
+                rhs=codes_in.bitcast(U8).bitcast(FP4X4),
                 rhs_scale=scales.bitcast(U8),
                 start=True,
                 stop=True,
             )
-        order_scales(0, 1)
-        order_scales(1, 1)
-        stage_scales(1, CHUNKS, sc_rest)
-        w_raw1 = keep.tile([P, 2, 2, 256], I32, name="w_raw1", tag="reused", align_bytes=64)
-        load_words(nc.sync, w_raw1, 1)
+        w_raw1 = keep.tile([P, 2, 2, 256], I32, name="w_raw1", tag="slot_w", align_bytes=64)
+        for m in range(2):
+            load_words(nc.sync, w_raw1[:, m], m, 1)
         move_scales(1)
+
+        got0 = keep.tile([P, CHUNK], I32, name="got0", tag="got", align_bytes=64)
+        gather_words(0, got0)
+        order_words(si_raw0[:], 1, 0)
+        sc_last = keep.tile([P, 128], I32, name="sc_last", tag="got", align_bytes=64)
+        gather_scales(3, sc_last, 0)
+        stage_scales(3, CHUNKS, sc_last)
+        move_scales(2)
 
         def power(j0, width, b, order):
             c, o = j0 // CHUNK, j0 % CHUNK
@@ -188,10 +199,10 @@ def tile_list_meltab_log_kernel(
                 for a in range(2):
                     nc.tensor.matmul_mx(
                         out=bank[:, lo : lo + width],
-                        lhsT=w_codes[:, m, b, t, a, :].bitcast(U8).bitcast(FP4X4),
-                        lhsT_scale=planes[ws][:, a, wlo + 32 * t : wlo + 32 * (t + 1)].bitcast(U8),
-                        rhs=parted[:, c, a, o : o + width].bitcast(U8).bitcast(FP4X4),
-                        rhs_scale=planes[ts][:, a, tlo + o // 4 : tlo + (o + width) // 4].bitcast(U8),
+                        lhsT=w_codes[m][b][:, 128 * t + 64 * a : 128 * t + 64 * (a + 1)].bitcast(U8).bitcast(FP4X4),
+                        lhsT_scale=planes[ws][:, a * WIDTHS[ws] + wlo + 32 * t : a * WIDTHS[ws] + wlo + 32 * (t + 1)].bitcast(U8),
+                        rhs=parted[c][a][:, o : o + width].bitcast(U8).bitcast(FP4X4),
+                        rhs_scale=planes[ts][:, a * WIDTHS[ts] + tlo + o // 4 : a * WIDTHS[ts] + tlo + (o + width) // 4].bitcast(U8),
                         start=(a == 0),
                         stop=(a == 1),
                     )
@@ -231,12 +242,12 @@ def tile_list_meltab_log_kernel(
         fb_plane = keep.tile([P, 2, N], U8, name="fb_plane", align_bytes=64)
 
         def prepare_fb():
-            fb_raw = keep.tile([P, 2, 4, N], F32, name="fb_raw", tag="reused", align_bytes=64)
+            fb_raw = keep.tile([P, 2, 4, N], F32, name="fb_raw", tag="slot_a", align_bytes=64)
             rows = fb.rearrange("(b q t e) n -> b e q t n", b=2, t=4, e=4)
             for b in range(2):
                 for e in range(4):
                     nc.sync.dma_start(out=fb_raw[e:P:4, b, :, :], in_=rows[b, e])
-            fb_bf = h_pool.tile([P, 2, N, 4], BF16, name="h", align_bytes=64)
+            fb_bf = keep.tile([P, 2, N, 4], BF16, name="fb_bf", align_bytes=64)
             for b in range(2):
                 nc.vector.tensor_tensor(
                     out=fb_bf[:, b].rearrange("p (c i) t -> p c t i", i=4),
@@ -280,23 +291,24 @@ def tile_list_meltab_log_kernel(
                     )
 
         by_t = [(t, m) for t in range(4) for m in range(2)]
-        waiting = None
+        done = []
         for c in range(CHUNKS):
             j0 = CHUNK * c
             low = power(j0, CHUNK, 0, by_t)
             if c == 0:
-                order_words(w_raw1, 0, 1)
-                order_words(w_raw1, 1, 1)
-            if waiting is not None and c > 1:
-                filters(*waiting)
+                order_words(w_raw1[:, 0], 0, 1)
+                order_words(w_raw1[:, 1], 1, 1)
+            if c == 2:
+                filters(*done[0])
             if c + 1 < CHUNKS:
                 got = keep.tile([P, CHUNK], I32, name="got%d" % (c + 1), tag="got", align_bytes=64)
                 gather_words(c + 1, got)
                 high = power(j0, CHUNK, 1, by_t)
-                if c == 1:
-                    filters(*waiting)
-                waiting = (j0, CHUNK, ((low[0], low[1], 0), (high[0], high[1], 0)))
+                if c == 2:
+                    filters(*done[1])
+                done.append((j0, CHUNK, ((low[0], low[1], 0), (high[0], high[1], 0))))
             else:
+                filters(*done[2])
                 pieces = []
                 for o, width in ((0, 256), (256, 128), (384, 128)):
                     high = power(j0 + o, width, 1, by_t)

@@ -51,13 +51,16 @@ def tile_list_meltab_log_kernel(
         w_codes = [
             [keep.tile([P, 4 * 2 * 64], I32, name="w_codes%d_%d" % (m, b), align_bytes=64) for b in range(2)] for m in range(2)
         ]
-        gn_rows = keep.tile([P, 2, P], F32, name="gn_rows")
+        gn_raw = keep.tile([2, 512], F32, name="gn_raw")
+        gn_rows = keep.tile([P, 4, P], F32, name="gn_rows")
         ident = keep.tile([P, P], F32, name="ident")
 
         nc.gpsimd.memset(gn_rows[:], 0.0)
         nc.gpsimd.memset(sc_win[32:64, :], 0)
         nc.vector.memset(sc_win[64:128, :], 0)
         nc.vector.memset(planes[0][:, 128:], 0)
+        nc.vector.memset(planes[1][:, 128:], 0)
+        nc.vector.memset(planes[2][:, 256:], 0)
 
         nc.scalar.dma_start(out=sc_win[0:32, :], in_=tab_scales.rearrange("a q t -> (a q) t").bitcast(I32))
         nc.sync.dma_start(offsets[:], offs)
@@ -71,10 +74,7 @@ def tile_list_meltab_log_kernel(
         for m in range(2):
             nc.scalar.dma_start(out=wsc_raw[:, m, :], in_=scales_in[m].rearrange("a q x -> (a q) x").bitcast(I32))
         load_words(nc.scalar, co_raw0[:], 0, 0)
-        nc.sync.dma_start(
-            out=gn_rows[0:4, :, :].rearrange("t b (q e) -> t (b q) e", e=4),
-            in_=gn.rearrange("(bq t e) -> t bq e", t=4, e=4),
-        )
+        nc.sync.dma_start(out=gn_raw[:], in_=gn.rearrange("(b x) -> b x", b=2))
         nc.scalar.dma_start(out=tab_win[:], in_=tab_words[0].rearrange("p t x -> p (t x)").bitcast(I32), max_dma_last_dim=4096)
         make_identity(nc, ident[:])
 
@@ -128,13 +128,14 @@ def tile_list_meltab_log_kernel(
         si_raw0 = keep.tile([P, 2, 256], I32, name="si_raw0", tag="slot_a", align_bytes=64)
         load_words(nc.sync, si_raw0[:], 1, 0)
         order_words(co_raw0[:], 0, 0)
-        nc.vector.memset(planes[1][:, 128:], 0)
-        nc.vector.memset(planes[2][:, 256:], 0)
 
         gain_ps = psum.tile([P, 512], F32, name="bank")
-        for b in range(2):
-            nc.tensor.transpose(gain_ps[:, P * b : P * (b + 1)], gn_rows[:, b, :], ident[:])
-        gain = gain_ps[:, 0 : 2 * P].rearrange("p (b x) -> p b x", b=2)[:, :, 0:4]
+        nc.vector.tensor_copy(
+            out=gn_rows[0:2].rearrange("b t (q e) -> b t q e", e=4), in_=gn_raw[:].rearrange("b (q t e) -> b t q e", t=4, e=4)
+        )
+        for t in range(4):
+            nc.tensor.transpose(gain_ps[:, P * t : P * (t + 1)], gn_rows[:, t, :], ident[:])
+        gain = gain_ps[:].rearrange("p (t x) -> p x t", t=4)[:, 0:2, :]
         mag = keep.tile([P, 2, 4], F32, name="mag")
         nc.scalar.activation(out=mag[:], in_=gain, func=ACT.Abs)
         mag8 = mag[:].rearrange("p b t -> p (b t)")
@@ -158,12 +159,9 @@ def tile_list_meltab_log_kernel(
         order_scales(0, 1)
         order_scales(1, 1)
         stage_scales(1, 2, sc_second)
-        sc_third = keep.tile([P, 128], I32, name="sc_third", tag="slot_s", align_bytes=64)
-        gather_scales(2, sc_third, 0)
-        stage_scales(2, 3, sc_third)
         warm_bank = psum.tile([P, 512], F32, name="bank")
         raw_codes = co_raw0[:, 0, :]
-        for codes_in, scales in [(raw_codes, planes[1][:, 0:128])] * 2 + [(tab_win[:, 0:256], sc_win[:, 0:128])] * 3:
+        for codes_in, scales in [(raw_codes, planes[1][:, 0:128])] * 2 + [(tab_win[:, 0:256], sc_win[:, 0:128])] * 2:
             nc.tensor.matmul_mx(
                 out=warm_bank[:],
                 lhsT=raw_codes[:, 0:64].bitcast(U8).bitcast(FP4X4),
@@ -181,9 +179,10 @@ def tile_list_meltab_log_kernel(
         got0 = keep.tile([P, CHUNK], I32, name="got0", tag="got", align_bytes=64)
         gather_words(0, got0)
         order_words(si_raw0[:], 1, 0)
-        sc_last = keep.tile([P, 128], I32, name="sc_last", tag="got", align_bytes=64)
-        gather_scales(3, sc_last, 0)
-        stage_scales(3, CHUNKS, sc_last)
+        sc_rest = keep.tile([P, 256], I32, name="sc_rest", tag="got", align_bytes=64)
+        for c in (2, 3):
+            gather_scales(c, sc_rest, c - 2)
+        stage_scales(2, CHUNKS, sc_rest)
         move_scales(2)
 
         def power(j0, width, b, order):

@@ -23,7 +23,7 @@ CHUNKS = J // CHUNK
 WIDTHS = (384, 384, 256)
 TAB_AT = ((0, 0), (1, 0), (2, 0), (2, 128))
 W_AT = (((0, 128), (1, 128)), ((0, 256), (1, 256)))
-ON_VECTOR = ((2, 3), (3, 3), (4, 3), (5, 3), (6, 3))
+ON_VECTOR = ((3, 3), (4, 3), (5, 3), (6, 3))
 SQRT_FLOOR = 2.0 ** -100
 
 
@@ -45,12 +45,8 @@ def tile_list_meltab_log_kernel(
         wsc_raw = keep.tile([32, 2, F // 4], I32, name="wsc_raw", tag="slot_w", align_bytes=64)
         co_raw0 = keep.tile([P, 2, 256], I32, name="co_raw0", align_bytes=64)
         planes = [keep.tile([P, 2 * WIDTHS[s]], I32, name="planes%d" % s, align_bytes=64) for s in range(3)]
-        parted = [
-            [keep.tile([P, CHUNK], U16, name="parted%d_%d" % (c, d), align_bytes=64) for d in range(2)] for c in range(CHUNKS)
-        ]
-        w_codes = [
-            [keep.tile([P, 4 * 2 * 64], I32, name="w_codes%d_%d" % (m, b), align_bytes=64) for b in range(2)] for m in range(2)
-        ]
+        parted = [keep.tile([P, 2 * CHUNK], U16, name="parted%d" % c, align_bytes=64) for c in range(CHUNKS)]
+        w_codes = {}
         gn_raw = keep.tile([2, 512], F32, name="gn_raw")
         gn_rows = keep.tile([P, 4, P], F32, name="gn_rows")
         ident = keep.tile([P, P], F32, name="ident")
@@ -103,12 +99,16 @@ def tile_list_meltab_log_kernel(
                 out=got[:].bitcast(U32), in_=tab_win[:].bitcast(U32).indirect(offsets[:, 32 * c : 32 * (c + 1)])
             )
             halves = got[:].bitcast(U16).rearrange("p (j d) -> p d j", d=2)
-            for d in range(2):
-                nc.vector.tensor_copy(out=parted[c][d][:], in_=halves[:, d, :])
+            if c == 0:
+                for d in range(2):
+                    nc.vector.tensor_copy(out=parted[c][:, CHUNK * d : CHUNK * (d + 1)], in_=halves[:, d, :])
+            else:
+                nc.vector.tensor_copy(out=parted[c][:].rearrange("p (d j) -> p d j", d=2), in_=halves)
 
-        def order_words(raw, m, b):
+        def order_words(raw, m, b, tag):
+            w_codes[m, b] = keep.tile([P, 4 * 2 * 64], I32, name="w_codes%d_%d" % (m, b), tag=tag, align_bytes=64)
             nc.vector.tensor_copy(
-                out=w_codes[m][b][:].rearrange("p (t x w) -> p t x w", t=4, w=2),
+                out=w_codes[m, b][:].rearrange("p (t x w) -> p t x w", t=4, w=2),
                 in_=raw.rearrange("p a (q t w) -> p t (a q) w", t=4, w=2),
             )
 
@@ -127,7 +127,7 @@ def tile_list_meltab_log_kernel(
         move_scales(0)
         si_raw0 = keep.tile([P, 2, 256], I32, name="si_raw0", tag="slot_a", align_bytes=64)
         load_words(nc.sync, si_raw0[:], 1, 0)
-        order_words(co_raw0[:], 0, 0)
+        order_words(co_raw0[:], 0, 0, "co0")
 
         gain_ps = psum.tile([P, 512], F32, name="bank")
         nc.vector.tensor_copy(
@@ -178,8 +178,8 @@ def tile_list_meltab_log_kernel(
 
         got0 = keep.tile([P, CHUNK], I32, name="got0", tag="got", align_bytes=64)
         gather_words(0, got0)
-        order_words(si_raw0[:], 1, 0)
-        sc_rest = keep.tile([P, 256], I32, name="sc_rest", tag="got", align_bytes=64)
+        order_words(si_raw0[:], 1, 0, "got")
+        sc_rest = keep.tile([P, 256], I32, name="sc_rest", tag="slot_a", align_bytes=64)
         for c in (2, 3):
             gather_scales(c, sc_rest, c - 2)
         stage_scales(2, CHUNKS, sc_rest)
@@ -198,9 +198,9 @@ def tile_list_meltab_log_kernel(
                 for a in range(2):
                     nc.tensor.matmul_mx(
                         out=bank[:, lo : lo + width],
-                        lhsT=w_codes[m][b][:, 128 * t + 64 * a : 128 * t + 64 * (a + 1)].bitcast(U8).bitcast(FP4X4),
+                        lhsT=w_codes[m, b][:, 128 * t + 64 * a : 128 * t + 64 * (a + 1)].bitcast(U8).bitcast(FP4X4),
                         lhsT_scale=planes[ws][:, a * WIDTHS[ws] + wlo + 32 * t : a * WIDTHS[ws] + wlo + 32 * (t + 1)].bitcast(U8),
-                        rhs=parted[c][a][:, o : o + width].bitcast(U8).bitcast(FP4X4),
+                        rhs=parted[c][:, CHUNK * a + o : CHUNK * a + o + width].bitcast(U8).bitcast(FP4X4),
                         rhs_scale=planes[ts][:, a * WIDTHS[ts] + tlo + o // 4 : a * WIDTHS[ts] + tlo + (o + width) // 4].bitcast(U8),
                         start=(a == 0),
                         stop=(a == 1),
@@ -241,7 +241,7 @@ def tile_list_meltab_log_kernel(
         fb_plane = keep.tile([P, 2, N], U8, name="fb_plane", align_bytes=64)
 
         def prepare_fb():
-            fb_raw = keep.tile([P, 2, 4, N], F32, name="fb_raw", tag="slot_a", align_bytes=64)
+            fb_raw = keep.tile([P, 2, 4, N], F32, name="fb_raw", tag="slot_s", align_bytes=64)
             rows = fb.rearrange("(b q t e) n -> b e q t n", b=2, t=4, e=4)
             for b in range(2):
                 for e in range(4):
@@ -295,12 +295,12 @@ def tile_list_meltab_log_kernel(
             j0 = CHUNK * c
             low = power(j0, CHUNK, 0, by_t)
             if c == 0:
-                order_words(w_raw1[:, 0], 0, 1)
-                order_words(w_raw1[:, 1], 1, 1)
+                order_words(w_raw1[:, 0], 0, 1, "co1")
+                order_words(w_raw1[:, 1], 1, 1, "si1")
             if c == 2:
                 filters(*done[0])
             if c + 1 < CHUNKS:
-                got = keep.tile([P, CHUNK], I32, name="got%d" % (c + 1), tag="got", align_bytes=64)
+                got = keep.tile([P, CHUNK], I32, name="got%d" % (c + 1), tag="slot_a", align_bytes=64)
                 gather_words(c + 1, got)
                 high = power(j0, CHUNK, 1, by_t)
                 if c == 2:

@@ -23,7 +23,7 @@ CHUNKS = J // CHUNK
 WIDTHS = (384, 384, 256)
 TAB_AT = ((0, 0), (1, 0), (2, 0), (2, 128))
 W_AT = (((0, 128), (1, 128)), ((0, 256), (1, 256)))
-ON_VECTOR = ((3, 3), (4, 3), (5, 3), (6, 3))
+ON_VECTOR = ((3, 3, 0), (4, 3, 0), (4, 3, 1), (5, 3, 0), (6, 3, 0))
 SQRT_FLOOR = 2.0 ** -100
 
 
@@ -33,8 +33,8 @@ def tile_list_meltab_log_kernel(
     nc = tc.nc
     with ExitStack() as ctx:
         keep = ctx.enter_context(tc.tile_pool(name="keep", bufs=1))
-        sq_pool = ctx.enter_context(tc.tile_pool(name="sq", bufs=3))
-        h_pool = ctx.enter_context(tc.tile_pool(name="h", bufs=2))
+        sq_pool = ctx.enter_context(tc.tile_pool(name="sq", bufs=4))
+        h_pool = ctx.enter_context(tc.tile_pool(name="h", bufs=3))
         hq_pool = ctx.enter_context(tc.tile_pool(name="hq", bufs=8))
         y_pool = ctx.enter_context(tc.tile_pool(name="y", bufs=4))
         psum = ctx.enter_context(tc.psum_pool(name="psum", bufs=8))
@@ -206,7 +206,7 @@ def tile_list_meltab_log_kernel(
                         stop=(a == 1),
                     )
                 scale = root[:, 4 * b + t : 4 * b + t + 1]
-                if width == CHUNK and m == 0 and (2 * c + b, t) in ON_VECTOR:
+                if width == CHUNK and (2 * c + b, t, m) in ON_VECTOR:
                     scaled = y_pool.tile([P, 512], F32, name="scaled")
                     nc.vector.tensor_scalar(out=scaled[:], in0=bank[:], scalar1=scale, scalar2=None, op0=ALU.mult)
                     nc.vector.tensor_tensor(out=sq[:, t, m, :], in0=scaled[:], in1=scaled[:], op=ALU.mult)

@@ -23,7 +23,7 @@ CHUNKS = J // CHUNK
 WIDTHS = (384, 384, 256)
 TAB_AT = ((0, 0), (1, 0), (2, 0), (2, 128))
 W_AT = (((0, 128), (1, 128)), ((0, 256), (1, 256)))
-ON_VECTOR = ((3, 3, 0), (4, 3, 0), (4, 3, 1), (5, 3, 0), (6, 3, 0))
+ON_VECTOR = ((3, 3, 0), (4, 3, 0), (5, 3, 0))
 SQRT_FLOOR = 2.0 ** -100
 
 
@@ -300,7 +300,7 @@ def tile_list_meltab_log_kernel(
             if c == 2:
                 filters(*done[0])
             if c + 1 < CHUNKS:
-                got = keep.tile([P, CHUNK], I32, name="got%d" % (c + 1), tag="slot_a", align_bytes=64)
+                got = keep.tile([P, CHUNK], I32, name="got%d" % (c + 1), tag=("slot_a", "slot_w")[c % 2], align_bytes=64)
                 gather_words(c + 1, got)
                 high = power(j0, CHUNK, 1, by_t)
                 if c == 2:

@@ -23,7 +23,7 @@ CHUNKS = J // CHUNK
 WIDTHS = (384, 384, 256)
 TAB_AT = ((0, 0), (1, 0), (2, 0), (2, 128))
 W_AT = (((0, 128), (1, 128)), ((0, 256), (1, 256)))
-ON_VECTOR = ((3, 3, 0), (4, 3, 0), (5, 3, 0))
+ON_VECTOR = ((3, 3, 0), (4, 3, 0), (4, 3, 1), (5, 3, 0))
 SQRT_FLOOR = 2.0 ** -100
 
 
@@ -223,9 +223,9 @@ def tile_list_meltab_log_kernel(
             for u in range(2):
                 cols = slice(half * u, half * (u + 1))
                 nc.vector.tensor_tensor(
-                    out=h[:, cols, :].rearrange("p (c i) t -> p c t i", i=4),
-                    in0=sq[:, :, 0, cols].rearrange("p t (c i) -> p c t i", i=4),
-                    in1=sq[:, :, 1, cols].rearrange("p t (c i) -> p c t i", i=4),
+                    out=h[:, cols, :].rearrange("p (c i) t -> p c t i", i=2),
+                    in0=sq[:, :, 0, cols].rearrange("p t (c i) -> p c t i", i=2),
+                    in1=sq[:, :, 1, cols].rearrange("p t (c i) -> p c t i", i=2),
                     op=ALU.add,
                 )
             for u in range(2):
@@ -249,9 +249,9 @@ def tile_list_meltab_log_kernel(
             fb_bf = keep.tile([P, 2, N, 4], BF16, name="fb_bf", align_bytes=64)
             for b in range(2):
                 nc.vector.tensor_tensor(
-                    out=fb_bf[:, b].rearrange("p (c i) t -> p c t i", i=4),
-                    in0=fb_raw[:, b].rearrange("p t (c i) -> p c t i", i=4),
-                    in1=sign[:, b, :].unsqueeze(1).unsqueeze(3).to_broadcast([P, N // 4, 4, 4]),
+                    out=fb_bf[:, b].rearrange("p (c i) t -> p c t i", i=2),
+                    in0=fb_raw[:, b].rearrange("p t (c i) -> p c t i", i=2),
+                    in1=sign[:, b, :].unsqueeze(1).unsqueeze(3).to_broadcast([P, N // 2, 4, 2]),
                     op=ALU.mult,
                 )
             nc.vector.quantize_mx(
@@ -307,11 +307,12 @@ def tile_list_meltab_log_kernel(
                     filters(*done[1])
                 done.append((j0, CHUNK, ((low[0], low[1], 0), (high[0], high[1], 0))))
             else:
-                filters(*done[2])
                 pieces = []
                 for o, width in ((0, 256), (256, 128), (384, 128)):
                     high = power(j0 + o, width, 1, by_t)
                     pieces.append((j0 + o, width, ((low[0], low[1], o), (high[0], high[1], 0))))
+                    if o == 0:
+                        filters(*done[2])
                 for piece in pieces:
                     filters(*piece)
             if c == 0:

@@ -20,10 +20,11 @@ ACT = mybir.ActivationFunctionType
 P = 128
 CHUNK = 512
 CHUNKS = J // CHUNK
-WIDTHS = (384, 384, 256)
-TAB_AT = ((0, 0), (1, 0), (2, 0), (2, 128))
-W_AT = (((0, 128), (1, 128)), ((0, 256), (1, 256)))
-ON_VECTOR = ((3, 3, 0), (4, 3, 0), (4, 3, 1), (5, 3, 0))
+WIDTHS = (384, 512, 128)
+TAB_AT = ((0, 0), (1, 0), (1, 128), (2, 0))
+W_AT = (((0, 128), (1, 256)), ((0, 256), (1, 384)))
+ON_VECTOR = ((3, 3, 0), (4, 3, 0), (5, 3, 0), (6, 3, 0))
+FILTERS_AFTER = {}
 SQRT_FLOOR = 2.0 ** -100
 
 
@@ -33,10 +34,11 @@ def tile_list_meltab_log_kernel(
     nc = tc.nc
     with ExitStack() as ctx:
         keep = ctx.enter_context(tc.tile_pool(name="keep", bufs=1))
-        sq_pool = ctx.enter_context(tc.tile_pool(name="sq", bufs=4))
+        sq_pool = ctx.enter_context(tc.tile_pool(name="sq", bufs=5))
         h_pool = ctx.enter_context(tc.tile_pool(name="h", bufs=3))
-        hq_pool = ctx.enter_context(tc.tile_pool(name="hq", bufs=8))
-        y_pool = ctx.enter_context(tc.tile_pool(name="y", bufs=4))
+        hq_pool = ctx.enter_context(tc.tile_pool(name="hq", bufs=9))
+        y_pool = ctx.enter_context(tc.tile_pool(name="y", bufs=8))
+        x_pool = ctx.enter_context(tc.tile_pool(name="x", bufs=2))
         psum = ctx.enter_context(tc.psum_pool(name="psum", bufs=8))
 
         offsets = keep.tile([P, J // 16], U16, name="offsets")
@@ -55,8 +57,6 @@ def tile_list_meltab_log_kernel(
         nc.gpsimd.memset(sc_win[32:64, :], 0)
         nc.vector.memset(sc_win[64:128, :], 0)
         nc.vector.memset(planes[0][:, 128:], 0)
-        nc.vector.memset(planes[1][:, 128:], 0)
-        nc.vector.memset(planes[2][:, 256:], 0)
 
         nc.scalar.dma_start(out=sc_win[0:32, :], in_=tab_scales.rearrange("a q t -> (a q) t").bitcast(I32))
         nc.sync.dma_start(offsets[:], offs)
@@ -73,12 +73,11 @@ def tile_list_meltab_log_kernel(
         nc.sync.dma_start(out=gn_raw[:], in_=gn.rearrange("(b x) -> b x", b=2))
         nc.scalar.dma_start(out=tab_win[:], in_=tab_words[0].rearrange("p t x -> p (t x)").bitcast(I32), max_dma_last_dim=4096)
         make_identity(nc, ident[:])
+        nc.gpsimd.memset(planes[1][:, 256:], 0)
+        nc.gpsimd.memset(planes[2][:, 128:], 0)
 
-        def gather_scales(c, sc_got, i):
-            nc.vector.tensor_copy(
-                out=sc_got[:].bitcast(U8)[:, CHUNK * i : CHUNK * (i + 1)],
-                in_=sc_win[:].bitcast(U8).indirect(offsets[:, 32 * c : 32 * (c + 1)]),
-            )
+        def gather_scales(c0, c1, sc_got):
+            nc.vector.tensor_copy(out=sc_got[:].bitcast(U8), in_=sc_win[:].bitcast(U8).indirect(offsets[:, 32 * c0 : 32 * c1]))
 
         def move_scales(s):
             w = WIDTHS[s]
@@ -108,19 +107,19 @@ def tile_list_meltab_log_kernel(
         def order_words(raw, m, b, tag):
             w_codes[m, b] = keep.tile([P, 4 * 2 * 64], I32, name="w_codes%d_%d" % (m, b), tag=tag, align_bytes=64)
             nc.vector.tensor_copy(
-                out=w_codes[m, b][:].rearrange("p (t x w) -> p t x w", t=4, w=2),
-                in_=raw.rearrange("p a (q t w) -> p t (a q) w", t=4, w=2),
+                out=w_codes[m, b][:].rearrange("p (t x w) -> p t x w", t=4, w=4),
+                in_=raw.rearrange("p a (r t w) -> p t (a r) w", t=4, w=4),
             )
 
         def order_scales(m, b):
             s, lo = W_AT[m][b]
             nc.vector.tensor_copy(
-                out=planes[s][0:32, lo : lo + 128].rearrange("p (t q) -> p t q", t=4),
-                in_=wsc_raw[:, m, 128 * b : 128 * (b + 1)].rearrange("p (q t) -> p t q", t=4),
+                out=planes[s][0:32, lo : lo + 128].rearrange("p (t r w) -> p t r w", t=4, w=2),
+                in_=wsc_raw[:, m, 128 * b : 128 * (b + 1)].rearrange("p (r t w) -> p t r w", t=4, w=2),
             )
 
         sc_first = keep.tile([P, 128], I32, name="sc_first", tag="slot_a", align_bytes=64)
-        gather_scales(0, sc_first, 0)
+        gather_scales(0, 1, sc_first)
         order_scales(0, 0)
         order_scales(1, 0)
         stage_scales(0, 1, sc_first)
@@ -131,7 +130,7 @@ def tile_list_meltab_log_kernel(
 
         gain_ps = psum.tile([P, 512], F32, name="bank")
         nc.vector.tensor_copy(
-            out=gn_rows[0:2].rearrange("b t (q e) -> b t q e", e=4), in_=gn_raw[:].rearrange("b (q t e) -> b t q e", t=4, e=4)
+            out=gn_rows[0:2].rearrange("b t (r e) -> b t r e", e=8), in_=gn_raw[:].rearrange("b (r t e) -> b t r e", t=4, e=8)
         )
         for t in range(4):
             nc.tensor.transpose(gain_ps[:, P * t : P * (t + 1)], gn_rows[:, t, :], ident[:])
@@ -154,11 +153,11 @@ def tile_list_meltab_log_kernel(
         root = keep.tile([P, 8], F32, name="root")
         nc.gpsimd.tensor_tensor(out=root[:], in0=root0[:], in1=mend[:], op=ALU.mult)
 
-        sc_second = keep.tile([P, 128], I32, name="sc_second", tag="slot_s", align_bytes=64)
-        gather_scales(1, sc_second, 0)
+        sc_second = keep.tile([P, 256], I32, name="sc_second", tag="slot_s", align_bytes=64)
+        gather_scales(1, 3, sc_second)
         order_scales(0, 1)
         order_scales(1, 1)
-        stage_scales(1, 2, sc_second)
+        stage_scales(1, 3, sc_second)
         warm_bank = psum.tile([P, 512], F32, name="bank")
         raw_codes = co_raw0[:, 0, :]
         for codes_in, scales in [(raw_codes, planes[1][:, 0:128])] * 2 + [(tab_win[:, 0:256], sc_win[:, 0:128])] * 2:
@@ -179,13 +178,8 @@ def tile_list_meltab_log_kernel(
         got0 = keep.tile([P, CHUNK], I32, name="got0", tag="got", align_bytes=64)
         gather_words(0, got0)
         order_words(si_raw0[:], 1, 0, "got")
-        sc_rest = keep.tile([P, 256], I32, name="sc_rest", tag="slot_a", align_bytes=64)
-        for c in (2, 3):
-            gather_scales(c, sc_rest, c - 2)
-        stage_scales(2, CHUNKS, sc_rest)
-        move_scales(2)
 
-        def power(j0, width, b, order):
+        def squares(j0, width, b, order):
             c, o = j0 // CHUNK, j0 % CHUNK
             ts, tlo = TAB_AT[c]
             sq = sq_pool.tile([P, 4, 2, width], F32, name="sq")
@@ -207,7 +201,7 @@ def tile_list_meltab_log_kernel(
                     )
                 scale = root[:, 4 * b + t : 4 * b + t + 1]
                 if width == CHUNK and (2 * c + b, t, m) in ON_VECTOR:
-                    scaled = y_pool.tile([P, 512], F32, name="scaled")
+                    scaled = x_pool.tile([P, 512], F32, name="scaled")
                     nc.vector.tensor_scalar(out=scaled[:], in0=bank[:], scalar1=scale, scalar2=None, op0=ALU.mult)
                     nc.vector.tensor_tensor(out=sq[:, t, m, :], in0=scaled[:], in1=scaled[:], op=ALU.mult)
                 elif width == CHUNK:
@@ -216,6 +210,9 @@ def tile_list_meltab_log_kernel(
                     nc.scalar.activation(
                         out=sq[:, t].rearrange("p m w -> p (m w)"), in_=bank[:, 0 : 2 * width], func=ACT.Square, scale=scale
                     )
+            return sq
+
+        def quantise(sq, width):
             h = h_pool.tile([P, width, 4], BF16, name="h", align_bytes=64)
             codes = hq_pool.tile([P, width], U32, name="codes", align_bytes=64)
             plane = hq_pool.tile([P, width], U8, name="plane", align_bytes=64)
@@ -242,10 +239,10 @@ def tile_list_meltab_log_kernel(
 
         def prepare_fb():
             fb_raw = keep.tile([P, 2, 4, N], F32, name="fb_raw", tag="slot_s", align_bytes=64)
-            rows = fb.rearrange("(b q t e) n -> b e q t n", b=2, t=4, e=4)
+            rows = fb.rearrange("(b r t e) n -> b t r e n", b=2, t=4, e=8)
             for b in range(2):
-                for e in range(4):
-                    nc.sync.dma_start(out=fb_raw[e:P:4, b, :, :], in_=rows[b, e])
+                for t in range(4):
+                    nc.sync.dma_start(out=fb_raw[:, b, t, :], in_=rows[b, t])
             fb_bf = keep.tile([P, 2, N, 4], BF16, name="fb_bf", align_bytes=64)
             for b in range(2):
                 nc.vector.tensor_tensor(
@@ -289,31 +286,47 @@ def tile_list_meltab_log_kernel(
                         in_=y[:, 0 : 2 * width].rearrange("p (i w) -> p i w", i=2),
                     )
 
+        def next_words(c):
+            got = keep.tile([P, CHUNK], I32, name="got%d" % c, tag=("slot_w", "slot_a")[c % 2], align_bytes=64)
+            gather_words(c, got)
+
         by_t = [(t, m) for t in range(4) for m in range(2)]
-        done = []
-        for c in range(CHUNKS):
-            j0 = CHUNK * c
-            low = power(j0, CHUNK, 0, by_t)
-            if c == 0:
+        by_m = [(t, m) for m in range(2) for t in range(4)]
+        done = {}
+        filtered = []
+
+        def whole(c):
+            filters(CHUNK * c, CHUNK, [done[2 * c + b] + (0,) for b in range(2)])
+            filtered.append(c)
+
+        waiting = None
+        for g in range(2 * CHUNKS - 1):
+            c, b = divmod(g, 2)
+            sq = squares(CHUNK * c, CHUNK, b, by_m if g == 0 else by_t)
+            if g == 0:
                 order_words(w_raw1[:, 0], 0, 1, "co1")
                 order_words(w_raw1[:, 1], 1, 1, "si1")
-            if c == 2:
-                filters(*done[0])
-            if c + 1 < CHUNKS:
-                got = keep.tile([P, CHUNK], I32, name="got%d" % (c + 1), tag=("slot_a", "slot_w")[c % 2], align_bytes=64)
-                gather_words(c + 1, got)
-                high = power(j0, CHUNK, 1, by_t)
-                if c == 2:
-                    filters(*done[1])
-                done.append((j0, CHUNK, ((low[0], low[1], 0), (high[0], high[1], 0))))
-            else:
-                pieces = []
-                for o, width in ((0, 256), (256, 128), (384, 128)):
-                    high = power(j0 + o, width, 1, by_t)
-                    pieces.append((j0 + o, width, ((low[0], low[1], o), (high[0], high[1], 0))))
-                    if o == 0:
-                        filters(*done[2])
-                for piece in pieces:
-                    filters(*piece)
-            if c == 0:
+            if b == 0 and c + 1 < CHUNKS:
+                next_words(c + 1)
+            if g == 1:
+                sc_last = keep.tile([P, 128], I32, name="sc_last", tag="slot_a", align_bytes=64)
+                gather_scales(3, 4, sc_last)
+                stage_scales(3, 4, sc_last)
+                move_scales(2)
+            if waiting is not None:
+                done[g - 1] = quantise(waiting, CHUNK)
+            if g == 2:
                 prepare_fb()
+            if g in FILTERS_AFTER:
+                whole(FILTERS_AFTER[g])
+            waiting = sq
+        j0 = J - CHUNK
+        last = [squares(j0, 256, 1, by_t)]
+        done[6] = quantise(waiting, CHUNK)
+        last.append(squares(j0 + 256, 256, 1, by_t))
+        pieces = [quantise(sq, 256) for sq in last]
+        for c in range(CHUNKS - 1):
+            if c not in filtered:
+                whole(c)
+        for u in range(2):
+            filters(j0 + 256 * u, 256, [done[6] + (256 * u,), pieces[u] + (0,)])

@@ -23,7 +23,7 @@ CHUNKS = J // CHUNK
 WIDTHS = (384, 512, 128)
 TAB_AT = ((0, 0), (1, 0), (1, 128), (2, 0))
 W_AT = (((0, 128), (1, 256)), ((0, 256), (1, 384)))
-ON_VECTOR = ((3, 3, 0), (4, 3, 0), (5, 3, 0), (6, 3, 0))
+ON_VECTOR = ()
 FILTERS_AFTER = {}
 SQRT_FLOOR = 2.0 ** -100
 

@@ -23,8 +23,8 @@ CHUNKS = J // CHUNK
 WIDTHS = (384, 512, 128)
 TAB_AT = ((0, 0), (1, 0), (1, 128), (2, 0))
 W_AT = (((0, 128), (1, 256)), ((0, 256), (1, 384)))
-ON_VECTOR = ()
-FILTERS_AFTER = {}
+ON_VECTOR = ((5, 3, 0), (6, 3, 0))
+FILTERS_AFTER = {5: 0}
 SQRT_FLOOR = 2.0 ** -100
 
 
@@ -37,7 +37,7 @@ def tile_list_meltab_log_kernel(
         sq_pool = ctx.enter_context(tc.tile_pool(name="sq", bufs=5))
         h_pool = ctx.enter_context(tc.tile_pool(name="h", bufs=3))
         hq_pool = ctx.enter_context(tc.tile_pool(name="hq", bufs=9))
-        y_pool = ctx.enter_context(tc.tile_pool(name="y", bufs=8))
+        y_pool = ctx.enter_context(tc.tile_pool(name="y", bufs=9))
         x_pool = ctx.enter_context(tc.tile_pool(name="x", bufs=2))
         psum = ctx.enter_context(tc.psum_pool(name="psum", bufs=8))
 
@@ -260,9 +260,9 @@ def tile_list_meltab_log_kernel(
         def filters(j0, width, halves):
             bank = None
             for i in range(2):
-                if width == CHUNK or i == 0:
+                if width == CHUNK or i == 0 or j0 + width == J:
                     bank = psum.tile([P, 512], F32, name="bank")
-                lo = 0 if width == CHUNK else i * width
+                lo = 0 if width == CHUNK or j0 + width == J else i * width
                 for b in range(2):
                     codes, plane, o = halves[b]
                     nc.tensor.matmul_mx(
@@ -278,6 +278,10 @@ def tile_list_meltab_log_kernel(
                     y = y_pool.tile([P, 512], F32, name="y")
                     nc.scalar.activation(out=y[:], in_=bank[:], func=ACT.Ln, bias=1.0)
                     nc.sync.dma_start(out=out[P * i : P * (i + 1), j0 : j0 + width], in_=y[:])
+                elif j0 + width == J:
+                    y = y_pool.tile([P, 512], F32, name="y")
+                    nc.scalar.activation(out=y[:, 0:width], in_=bank[:, 0:width], func=ACT.Ln, bias=1.0)
+                    nc.sync.dma_start(out=out[P * i : P * (i + 1), j0 : j0 + width], in_=y[:, 0:width])
                 elif i == 1:
                     y = y_pool.tile([P, 512], F32, name="y")
                     nc.scalar.activation(out=y[:, 0 : 2 * width], in_=bank[:, 0 : 2 * width], func=ACT.Ln, bias=1.0)

@@ -25,7 +25,7 @@ TAB_AT = ((0, 0), (1, 0), (1, 128), (2, 0))
 W_AT = (((0, 128), (1, 256)), ((0, 256), (1, 384)))
 ON_VECTOR = ((5, 3, 0), (6, 3, 0))
 FILTERS_AFTER = {5: 0}
-SQRT_FLOOR = 2.0 ** -100
+SQRT_FLOOR = 2.0 ** -80
 
 
 def tile_list_meltab_log_kernel(
@@ -258,11 +258,9 @@ def tile_list_meltab_log_kernel(
             )
 
         def filters(j0, width, halves):
-            bank = None
             for i in range(2):
-                if width == CHUNK or i == 0 or j0 + width == J:
-                    bank = psum.tile([P, 512], F32, name="bank")
-                lo = 0 if width == CHUNK or j0 + width == J else i * width
+                bank = psum.tile([P, 512], F32, name="bank")
+                lo = 0
                 for b in range(2):
                     codes, plane, o = halves[b]
                     nc.tensor.matmul_mx(
@@ -274,21 +272,30 @@ def tile_list_meltab_log_kernel(
                         start=(b == 0),
                         stop=(b == 1),
                     )
-                if width == CHUNK:
-                    y = y_pool.tile([P, 512], F32, name="y")
-                    nc.scalar.activation(out=y[:], in_=bank[:], func=ACT.Ln, bias=1.0)
-                    nc.sync.dma_start(out=out[P * i : P * (i + 1), j0 : j0 + width], in_=y[:])
-                elif j0 + width == J:
-                    y = y_pool.tile([P, 512], F32, name="y")
-                    nc.scalar.activation(out=y[:, 0:width], in_=bank[:, 0:width], func=ACT.Ln, bias=1.0)
-                    nc.sync.dma_start(out=out[P * i : P * (i + 1), j0 : j0 + width], in_=y[:, 0:width])
-                elif i == 1:
-                    y = y_pool.tile([P, 512], F32, name="y")
-                    nc.scalar.activation(out=y[:, 0 : 2 * width], in_=bank[:, 0 : 2 * width], func=ACT.Ln, bias=1.0)
-                    nc.sync.dma_start(
-                        out=out[:, j0 : j0 + width].rearrange("(i p) w -> p i w", p=P),
-                        in_=y[:, 0 : 2 * width].rearrange("p (i w) -> p i w", i=2),
+                y = y_pool.tile([P, 512], F32, name="y")
+                nc.scalar.activation(out=y[:], in_=bank[:], func=ACT.Ln, bias=1.0)
+                nc.sync.dma_start(out=out[P * i : P * (i + 1), j0 : j0 + width], in_=y[:])
+
+        def filters_one_bank(j0, width, halves):
+            bank = psum.tile([P, 512], F32, name="bank")
+            for b in range(2):
+                codes, plane, o = halves[b]
+                for i in range(2):
+                    nc.tensor.matmul_mx(
+                        out=bank[:, width * i : width * (i + 1)],
+                        lhsT=fb_codes[:, b, P * i : P * (i + 1)].bitcast(FP8X4),
+                        lhsT_scale=fb_plane[:, b, P * i : P * (i + 1)],
+                        rhs=codes[:, o : o + width].bitcast(FP8X4),
+                        rhs_scale=plane[:, o : o + width],
+                        start=(b + i == 0),
+                        stop=(b + i == 2),
                     )
+            y = y_pool.tile([P, 512], F32, name="y")
+            nc.scalar.activation(out=y[:, 0 : 2 * width], in_=bank[:, 0 : 2 * width], func=ACT.Ln, bias=1.0)
+            nc.sync.dma_start(
+                out=out[:, j0 : j0 + width].rearrange("(i p) w -> p i w", p=P),
+                in_=y[:, 0 : 2 * width].rearrange("p (i w) -> p i w", i=2),
+            )
 
         def next_words(c):
             got = keep.tile([P, CHUNK], I32, name="got%d" % c, tag=("slot_w", "slot_a")[c % 2], align_bytes=64)
@@ -332,5 +339,6 @@ def tile_list_meltab_log_kernel(
         for c in range(CHUNKS - 1):
             if c not in filtered:
                 whole(c)
-        for u in range(2):
-            filters(j0 + 256 * u, 256, [done[6] + (256 * u,), pieces[u] + (0,)])
+        filters_one_bank(j0, 256, [done[6] + (0,), pieces[0] + (0,)])
+        for o in (0, 128):
+            filters_one_bank(j0 + 256 + o, 128, [done[6] + (256 + o,), pieces[1] + (o,)])

@@ -39,12 +39,13 @@ def tile_list_meltab_log_kernel(
         hq_pool = ctx.enter_context(tc.tile_pool(name="hq", bufs=9))
         y_pool = ctx.enter_context(tc.tile_pool(name="y", bufs=9))
         x_pool = ctx.enter_context(tc.tile_pool(name="x", bufs=2))
+        head = ctx.enter_context(tc.tile_pool(name="head", bufs=1))
         psum = ctx.enter_context(tc.psum_pool(name="psum", bufs=8))
 
         offsets = keep.tile([P, J // 16], U16, name="offsets")
         tab_win = keep.tile([P, T], I32, name="tab_win", align_bytes=64)
         sc_win = keep.tile([P, T // 4], I32, name="sc_win", align_bytes=64)
-        wsc_raw = keep.tile([32, 2, F // 4], I32, name="wsc_raw", tag="slot_w", align_bytes=64)
+        wsc_raw = head.tile([32, 2, F // 4], I32, name="wsc_raw", offset=1024, align_bytes=64)
         co_raw0 = keep.tile([P, 2, 256], I32, name="co_raw0", align_bytes=64)
         planes = [keep.tile([P, 2 * WIDTHS[s]], I32, name="planes%d" % s, align_bytes=64) for s in range(3)]
         parted = [keep.tile([P, 2 * CHUNK], U16, name="parted%d" % c, align_bytes=64) for c in range(CHUNKS)]
@@ -105,7 +106,10 @@ def tile_list_meltab_log_kernel(
                 nc.vector.tensor_copy(out=parted[c][:].rearrange("p (d j) -> p d j", d=2), in_=halves)
 
         def order_words(raw, m, b, tag):
-            w_codes[m, b] = keep.tile([P, 4 * 2 * 64], I32, name="w_codes%d_%d" % (m, b), tag=tag, align_bytes=64)
+            if tag is None:
+                w_codes[m, b] = head.tile([P, 4 * 2 * 64], I32, name="w_codes%d_%d" % (m, b), offset=7168, align_bytes=64)
+            else:
+                w_codes[m, b] = keep.tile([P, 4 * 2 * 64], I32, name="w_codes%d_%d" % (m, b), tag=tag, align_bytes=64)
             nc.vector.tensor_copy(
                 out=w_codes[m, b][:].rearrange("p (t x w) -> p t x w", t=4, w=4),
                 in_=raw.rearrange("p a (r t w) -> p t (a r) w", t=4, w=4),
@@ -170,14 +174,17 @@ def tile_list_meltab_log_kernel(
                 start=True,
                 stop=True,
             )
-        w_raw1 = keep.tile([P, 2, 2, 256], I32, name="w_raw1", tag="slot_w", align_bytes=64)
+        w_raw1 = [head.tile([P, 2, 256], I32, name="w_raw1_%d" % m, offset=2048 * m, align_bytes=64) for m in range(2)]
         for m in range(2):
-            load_words(nc.sync, w_raw1[:, m], m, 1)
+            load_words(nc.sync, w_raw1[m][:], m, 1)
         move_scales(1)
 
-        got0 = keep.tile([P, CHUNK], I32, name="got0", tag="got", align_bytes=64)
+        got0 = head.tile([P, CHUNK], I32, name="got0", offset=6144, align_bytes=64)
         gather_words(0, got0)
-        order_words(si_raw0[:], 1, 0, "got")
+        sc_last = head.tile([P, 128], I32, name="sc_last", offset=6144, align_bytes=64)
+        gather_scales(3, 4, sc_last)
+        order_words(si_raw0[:], 1, 0, None)
+        stage_scales(3, 4, sc_last)
 
         def squares(j0, width, b, order):
             c, o = j0 // CHUNK, j0 % CHUNK
@@ -202,8 +209,10 @@ def tile_list_meltab_log_kernel(
                 scale = root[:, 4 * b + t : 4 * b + t + 1]
                 if width == CHUNK and (2 * c + b, t, m) in ON_VECTOR:
                     scaled = x_pool.tile([P, 512], F32, name="scaled")
-                    nc.vector.tensor_scalar(out=scaled[:], in0=bank[:], scalar1=scale, scalar2=None, op0=ALU.mult)
-                    nc.vector.tensor_tensor(out=sq[:, t, m, :], in0=scaled[:], in1=scaled[:], op=ALU.mult)
+                    for cols in (slice(0, 256), slice(256, 512)):
+                        nc.vector.tensor_scalar(out=scaled[:, cols], in0=bank[:, cols], scalar1=scale, scalar2=None, op0=ALU.mult)
+                    for cols in (slice(0, 256), slice(256, 512)):
+                        nc.vector.tensor_tensor(out=sq[:, t, m, cols], in0=scaled[:, cols], in1=scaled[:, cols], op=ALU.mult)
                 elif width == CHUNK:
                     nc.scalar.activation(out=sq[:, t, m, :], in_=bank[:], func=ACT.Square, scale=scale)
                 elif m == 1:
@@ -251,11 +260,10 @@ def tile_list_meltab_log_kernel(
                     in1=sign[:, b, :].unsqueeze(1).unsqueeze(3).to_broadcast([P, N // 2, 4, 2]),
                     op=ALU.mult,
                 )
-            nc.vector.quantize_mx(
-                out=fb_codes[:].rearrange("p b n -> p (b n)").bitcast(FP8X4),
-                scales=fb_plane[:].rearrange("p b n -> p (b n)"),
-                in_=fb_bf[:].rearrange("p b n t -> p (b n t)"),
-            )
+            for b in range(2):
+                nc.vector.quantize_mx(
+                    out=fb_codes[:, b].bitcast(FP8X4), scales=fb_plane[:, b], in_=fb_bf[:, b].rearrange("p n t -> p (n t)")
+                )
 
         def filters(j0, width, halves):
             for i in range(2):
@@ -298,7 +306,10 @@ def tile_list_meltab_log_kernel(
             )
 
         def next_words(c):
-            got = keep.tile([P, CHUNK], I32, name="got%d" % c, tag=("slot_w", "slot_a")[c % 2], align_bytes=64)
+            if c == 1:
+                got = keep.tile([P, CHUNK], I32, name="got1", tag="slot_a", align_bytes=64)
+            else:
+                got = head.tile([P, CHUNK], I32, name="got%d" % c, offset=(1024, 3072)[c - 2], align_bytes=64)
             gather_words(c, got)
 
         by_t = [(t, m) for t in range(4) for m in range(2)]
@@ -315,14 +326,11 @@ def tile_list_meltab_log_kernel(
             c, b = divmod(g, 2)
             sq = squares(CHUNK * c, CHUNK, b, by_m if g == 0 else by_t)
             if g == 0:
-                order_words(w_raw1[:, 0], 0, 1, "co1")
-                order_words(w_raw1[:, 1], 1, 1, "si1")
+                order_words(w_raw1[0][:], 0, 1, "co1")
+                order_words(w_raw1[1][:], 1, 1, "si1")
             if b == 0 and c + 1 < CHUNKS:
                 next_words(c + 1)
             if g == 1:
-                sc_last = keep.tile([P, 128], I32, name="sc_last", tag="slot_a", align_bytes=64)
-                gather_scales(3, 4, sc_last)
-                stage_scales(3, 4, sc_last)
                 move_scales(2)
             if waiting is not None:
                 done[g - 1] = quantise(waiting, CHUNK)

@@ -45,7 +45,7 @@ def tile_list_meltab_log_kernel(
         offsets = keep.tile([P, J // 16], U16, name="offsets")
         tab_win = keep.tile([P, T], I32, name="tab_win", align_bytes=64)
         sc_win = keep.tile([P, T // 4], I32, name="sc_win", align_bytes=64)
-        wsc_raw = head.tile([32, 2, F // 4], I32, name="wsc_raw", offset=1024, align_bytes=64)
+        wsc_raw = head.tile([32, 2, F // 4], I32, name="wsc_raw", offset=2048, align_bytes=64)
         co_raw0 = keep.tile([P, 2, 256], I32, name="co_raw0", align_bytes=64)
         planes = [keep.tile([P, 2 * WIDTHS[s]], I32, name="planes%d" % s, align_bytes=64) for s in range(3)]
         parted = [keep.tile([P, 2 * CHUNK], U16, name="parted%d" % c, align_bytes=64) for c in range(CHUNKS)]
@@ -174,7 +174,7 @@ def tile_list_meltab_log_kernel(
                 start=True,
                 stop=True,
             )
-        w_raw1 = [head.tile([P, 2, 256], I32, name="w_raw1_%d" % m, offset=2048 * m, align_bytes=64) for m in range(2)]
+        w_raw1 = [head.tile([P, 2, 256], I32, name="w_raw1_%d" % m, offset=1024 + 2048 * m, align_bytes=64) for m in range(2)]
         for m in range(2):
             load_words(nc.sync, w_raw1[m][:], m, 1)
         move_scales(1)
@@ -221,8 +221,11 @@ def tile_list_meltab_log_kernel(
                     )
             return sq
 
-        def quantise(sq, width):
-            h = h_pool.tile([P, width, 4], BF16, name="h", align_bytes=64)
+        def quantise(sq, width, first=False):
+            if first:
+                h = head.tile([P, width, 4], BF16, name="h0", offset=11264, align_bytes=64)
+            else:
+                h = h_pool.tile([P, width, 4], BF16, name="h", align_bytes=64)
             codes = hq_pool.tile([P, width], U32, name="codes", align_bytes=64)
             plane = hq_pool.tile([P, width], U8, name="plane", align_bytes=64)
             half = width // 2
@@ -252,17 +255,20 @@ def tile_list_meltab_log_kernel(
             for b in range(2):
                 for t in range(4):
                     nc.sync.dma_start(out=fb_raw[:, b, t, :], in_=rows[b, t])
-            fb_bf = keep.tile([P, 2, N, 4], BF16, name="fb_bf", align_bytes=64)
+            fb_bf = [
+                head.tile([P, N, 4], BF16, name="fb_bf0", offset=12288, align_bytes=64),
+                keep.tile([P, N, 4], BF16, name="fb_bf1", align_bytes=64),
+            ]
             for b in range(2):
-                nc.vector.tensor_tensor(
-                    out=fb_bf[:, b].rearrange("p (c i) t -> p c t i", i=2),
+                (nc.gpsimd, nc.vector)[b].tensor_tensor(
+                    out=fb_bf[b][:].rearrange("p (c i) t -> p c t i", i=2),
                     in0=fb_raw[:, b].rearrange("p t (c i) -> p c t i", i=2),
                     in1=sign[:, b, :].unsqueeze(1).unsqueeze(3).to_broadcast([P, N // 2, 4, 2]),
                     op=ALU.mult,
                 )
             for b in range(2):
                 nc.vector.quantize_mx(
-                    out=fb_codes[:, b].bitcast(FP8X4), scales=fb_plane[:, b], in_=fb_bf[:, b].rearrange("p n t -> p (n t)")
+                    out=fb_codes[:, b].bitcast(FP8X4), scales=fb_plane[:, b], in_=fb_bf[b][:].rearrange("p n t -> p (n t)")
                 )
 
         def filters(j0, width, halves):
@@ -309,7 +315,7 @@ def tile_list_meltab_log_kernel(
             if c == 1:
                 got = keep.tile([P, CHUNK], I32, name="got1", tag="slot_a", align_bytes=64)
             else:
-                got = head.tile([P, CHUNK], I32, name="got%d" % c, offset=(1024, 3072)[c - 2], align_bytes=64)
+                got = head.tile([P, CHUNK], I32, name="got%d" % c, offset=(10240, 14336)[c - 2], align_bytes=64)
             gather_words(c, got)
 
         by_t = [(t, m) for t in range(4) for m in range(2)]
@@ -328,13 +334,15 @@ def tile_list_meltab_log_kernel(
             if g == 0:
                 order_words(w_raw1[0][:], 0, 1, "co1")
                 order_words(w_raw1[1][:], 1, 1, "si1")
-            if b == 0 and c + 1 < CHUNKS:
-                next_words(c + 1)
+            if g == 0:
+                next_words(1)
             if g == 1:
                 move_scales(2)
             if waiting is not None:
-                done[g - 1] = quantise(waiting, CHUNK)
-            if g == 2:
+                done[g - 1] = quantise(waiting, CHUNK, g == 1)
+            if g == 1:
+                next_words(2)
+                next_words(3)
                 prepare_fb()
             if g in FILTERS_AFTER:
                 whole(FILTERS_AFTER[g])

@@ -23,7 +23,7 @@ CHUNKS = J // CHUNK
 WIDTHS = (384, 512, 128)
 TAB_AT = ((0, 0), (1, 0), (1, 128), (2, 0))
 W_AT = (((0, 128), (1, 256)), ((0, 256), (1, 384)))
-ON_VECTOR = ((5, 3, 0), (6, 3, 0))
+ON_VECTOR = ((5, 1, 1), (6, 1, 1))
 FILTERS_AFTER = {5: 0}
 SQRT_FLOOR = 2.0 ** -80
 
@@ -186,6 +186,8 @@ def tile_list_meltab_log_kernel(
         order_words(si_raw0[:], 1, 0, None)
         stage_scales(3, 4, sc_last)
 
+        on_vector = []
+
         def squares(j0, width, b, order):
             c, o = j0 // CHUNK, j0 % CHUNK
             ts, tlo = TAB_AT[c]
@@ -208,11 +210,7 @@ def tile_list_meltab_log_kernel(
                     )
                 scale = root[:, 4 * b + t : 4 * b + t + 1]
                 if width == CHUNK and (2 * c + b, t, m) in ON_VECTOR:
-                    scaled = x_pool.tile([P, 512], F32, name="scaled")
-                    for cols in (slice(0, 256), slice(256, 512)):
-                        nc.vector.tensor_scalar(out=scaled[:, cols], in0=bank[:, cols], scalar1=scale, scalar2=None, op0=ALU.mult)
-                    for cols in (slice(0, 256), slice(256, 512)):
-                        nc.vector.tensor_tensor(out=sq[:, t, m, cols], in0=scaled[:, cols], in1=scaled[:, cols], op=ALU.mult)
+                    on_vector.append((bank, scale, sq[:, t, m, :]))
                 elif width == CHUNK:
                     nc.scalar.activation(out=sq[:, t, m, :], in_=bank[:], func=ACT.Square, scale=scale)
                 elif m == 1:
@@ -221,24 +219,28 @@ def tile_list_meltab_log_kernel(
                     )
             return sq
 
-        def quantise(sq, width, first=False):
+        def add_squares(sq, width, parts, first=False):
             if first:
                 h = head.tile([P, width, 4], BF16, name="h0", offset=11264, align_bytes=64)
             else:
                 h = h_pool.tile([P, width, 4], BF16, name="h", align_bytes=64)
-            codes = hq_pool.tile([P, width], U32, name="codes", align_bytes=64)
-            plane = hq_pool.tile([P, width], U8, name="plane", align_bytes=64)
-            half = width // 2
-            for u in range(2):
-                cols = slice(half * u, half * (u + 1))
+            step = width // parts
+            for u in range(parts):
+                cols = slice(step * u, step * (u + 1))
                 nc.vector.tensor_tensor(
                     out=h[:, cols, :].rearrange("p (c i) t -> p c t i", i=2),
                     in0=sq[:, :, 0, cols].rearrange("p t (c i) -> p c t i", i=2),
                     in1=sq[:, :, 1, cols].rearrange("p t (c i) -> p c t i", i=2),
                     op=ALU.add,
                 )
-            for u in range(2):
-                cols = slice(half * u, half * (u + 1))
+            return h
+
+        def quantise(h, width, parts):
+            codes = hq_pool.tile([P, width], U32, name="codes", align_bytes=64)
+            plane = hq_pool.tile([P, width], U8, name="plane", align_bytes=64)
+            step = width // parts
+            for u in range(parts):
+                cols = slice(step * u, step * (u + 1))
                 nc.vector.quantize_mx(
                     out=codes[:, cols].bitcast(FP8X4),
                     scales=plane[:, cols],
@@ -338,8 +340,15 @@ def tile_list_meltab_log_kernel(
                 next_words(1)
             if g == 1:
                 move_scales(2)
-            if waiting is not None:
-                done[g - 1] = quantise(waiting, CHUNK, g == 1)
+            if on_vector:
+                bank, scale, square = on_vector.pop()
+                h = add_squares(waiting, CHUNK, 1)
+                scaled = x_pool.tile([P, 512], F32, name="scaled")
+                nc.vector.tensor_scalar(out=scaled[:], in0=bank[:], scalar1=scale, scalar2=None, op0=ALU.mult)
+                done[g - 1] = quantise(h, CHUNK, 1)
+                nc.vector.tensor_tensor(out=square, in0=scaled[:], in1=scaled[:], op=ALU.mult)
+            elif waiting is not None:
+                done[g - 1] = quantise(add_squares(waiting, CHUNK, 2, g == 1), CHUNK, 2)
             if g == 1:
                 next_words(2)
                 next_words(3)
@@ -348,10 +357,11 @@ def tile_list_meltab_log_kernel(
                 whole(FILTERS_AFTER[g])
             waiting = sq
         j0 = J - CHUNK
-        last = [squares(j0, 256, 1, by_t)]
-        done[6] = quantise(waiting, CHUNK)
-        last.append(squares(j0 + 256, 256, 1, by_t))
-        pieces = [quantise(sq, 256) for sq in last]
+        last = [squares(j0 + 256 * u, 256, 1, by_t) for u in range(2)]
+        h6 = add_squares(waiting, CHUNK, 1)
+        h7 = add_squares(last[0], 256, 1)
+        done[6] = quantise(h6, CHUNK, 1)
+        pieces = [quantise(h7, 256, 1), quantise(add_squares(last[1], 256, 2), 256, 2)]
         for c in range(CHUNKS - 1):
             if c not in filtered:
                 whole(c)

from contextlib import ExitStack

import concourse.mybir as mybir
from concourse.masks import make_identity

K, F, N, T, J = 1024, 1024, 256, 4096, 2048
FLOPS = 2 * (2 * K * F * J + F * N * J)

F32 = mybir.dt.float32
BF16 = mybir.dt.bfloat16
I32 = mybir.dt.int32
U32 = mybir.dt.uint32
U16 = mybir.dt.uint16
U8 = mybir.dt.uint8
FP4X4 = mybir.dt.float4_e2m1fn_x4
FP8X4 = mybir.dt.float8_e4m3fn_x4
ALU = mybir.AluOpType
ACT = mybir.ActivationFunctionType

P = 128
CHUNK = 512
CHUNKS = J // CHUNK
WIDTHS = (384, 512, 128)
TAB_AT = ((0, 0), (1, 0), (1, 128), (2, 0))
W_AT = (((0, 128), (1, 256)), ((0, 256), (1, 384)))
ON_VECTOR = ((5, 1, 1), (6, 1, 1))
FILTERS_AFTER = {5: 0}
SQRT_FLOOR = 2.0 ** -80


def tile_list_meltab_log_kernel(
    tc, tab_words, tab_scales, co_words, co_scales, si_words, si_scales, gn, fb, offs, out
):
    nc = tc.nc
    with ExitStack() as ctx:
        keep = ctx.enter_context(tc.tile_pool(name="keep", bufs=1))
        sq_pool = ctx.enter_context(tc.tile_pool(name="sq", bufs=5))
        h_pool = ctx.enter_context(tc.tile_pool(name="h", bufs=3))
        hq_pool = ctx.enter_context(tc.tile_pool(name="hq", bufs=9))
        y_pool = ctx.enter_context(tc.tile_pool(name="y", bufs=9))
        x_pool = ctx.enter_context(tc.tile_pool(name="x", bufs=2))
        head = ctx.enter_context(tc.tile_pool(name="head", bufs=1))
        psum = ctx.enter_context(tc.psum_pool(name="psum", bufs=8))

        offsets = keep.tile([P, J // 16], U16, name="offsets")
        tab_win = keep.tile([P, T], I32, name="tab_win", align_bytes=64)
        sc_win = keep.tile([P, T // 4], I32, name="sc_win", align_bytes=64)
        wsc_raw = head.tile([32, 2, F // 4], I32, name="wsc_raw", offset=2048, align_bytes=64)
        co_raw0 = keep.tile([P, 2, 256], I32, name="co_raw0", align_bytes=64)
        planes = [keep.tile([P, 2 * WIDTHS[s]], I32, name="planes%d" % s, align_bytes=64) for s in range(3)]
        parted = [keep.tile([P, 2 * CHUNK], U16, name="parted%d" % c, align_bytes=64) for c in range(CHUNKS)]
        w_codes = {}
        gn_raw = keep.tile([2, 512], F32, name="gn_raw")
        gn_rows = keep.tile([P, 4, P], F32, name="gn_rows")
        ident = keep.tile([P, P], F32, name="ident")

        nc.gpsimd.memset(gn_rows[:], 0.0)
        nc.gpsimd.memset(sc_win[32:64, :], 0)
        nc.vector.memset(sc_win[64:128, :], 0)
        nc.vector.memset(planes[0][:, 128:], 0)

        nc.scalar.dma_start(out=sc_win[0:32, :], in_=tab_scales.rearrange("a q t -> (a q) t").bitcast(I32))
        nc.sync.dma_start(offsets[:], offs)
        words_in = (co_words, si_words)
        scales_in = (co_scales, si_scales)

        def load_words(queue, raw, m, b):
            src = words_in[m][:, :, 1024 * b : 1024 * (b + 1)].rearrange("a p x -> p a x").bitcast(I32)
            queue.dma_start(out=raw, in_=src)

        for m in range(2):
            nc.scalar.dma_start(out=wsc_raw[:, m, :], in_=scales_in[m].rearrange("a q x -> (a q) x").bitcast(I32))
        load_words(nc.scalar, co_raw0[:], 0, 0)
        nc.sync.dma_start(out=gn_raw[:], in_=gn.rearrange("(b x) -> b x", b=2))
        nc.scalar.dma_start(out=tab_win[:], in_=tab_words[0].rearrange("p t x -> p (t x)").bitcast(I32), max_dma_last_dim=4096)
        make_identity(nc, ident[:])
        nc.gpsimd.memset(planes[1][:, 256:], 0)
        nc.gpsimd.memset(planes[2][:, 128:], 0)

        def gather_scales(c0, c1, sc_got):
            nc.vector.tensor_copy(out=sc_got[:].bitcast(U8), in_=sc_win[:].bitcast(U8).indirect(offsets[:, 32 * c0 : 32 * c1]))

        def move_scales(s):
            w = WIDTHS[s]
            for a in range(2):
                for q in range(4):
                    if a or q:
                        nc.sync.dma_start(
                            out=planes[s][32 * q : 32 * q + 4, a * w : (a + 1) * w],
                            in_=planes[s][16 * a + 4 * q : 16 * a + 4 * q + 4, 0:w],
                        )

        def stage_scales(c0, c1, sc_got):
            s, lo = TAB_AT[c0]
            nc.vector.tensor_copy(out=planes[s][:, lo : lo + 128 * (c1 - c0)], in_=sc_got[:])

        def gather_words(c, got):
            nc.vector.tensor_copy(
                out=got[:].bitcast(U32), in_=tab_win[:].bitcast(U32).indirect(offsets[:, 32 * c : 32 * (c + 1)])
            )
            halves = got[:].bitcast(U16).rearrange("p (j d) -> p d j", d=2)
            if c == 0:
                for d in range(2):
                    nc.vector.tensor_copy(out=parted[c][:, CHUNK * d : CHUNK * (d + 1)], in_=halves[:, d, :])
            else:
                nc.vector.tensor_copy(out=parted[c][:].rearrange("p (d j) -> p d j", d=2), in_=halves)

        def order_words(raw, m, b, tag):
            if tag is None:
                w_codes[m, b] = head.tile([P, 4 * 2 * 64], I32, name="w_codes%d_%d" % (m, b), offset=7168, align_bytes=64)
            else:
                w_codes[m, b] = keep.tile([P, 4 * 2 * 64], I32, name="w_codes%d_%d" % (m, b), tag=tag, align_bytes=64)
            nc.vector.tensor_copy(
                out=w_codes[m, b][:].rearrange("p (t x w) -> p t x w", t=4, w=4),
                in_=raw.rearrange("p a (r t w) -> p t (a r) w", t=4, w=4),
            )

        def order_scales(m, b):
            s, lo = W_AT[m][b]
            nc.vector.tensor_copy(
                out=planes[s][0:32, lo : lo + 128].rearrange("p (t r w) -> p t r w", t=4, w=2),
                in_=wsc_raw[:, m, 128 * b : 128 * (b + 1)].rearrange("p (r t w) -> p t r w", t=4, w=2),
            )

        sc_first = keep.tile([P, 128], I32, name="sc_first", tag="slot_a", align_bytes=64)
        gather_scales(0, 1, sc_first)
        order_scales(0, 0)
        order_scales(1, 0)
        stage_scales(0, 1, sc_first)
        move_scales(0)
        si_raw0 = keep.tile([P, 2, 256], I32, name="si_raw0", tag="slot_a", align_bytes=64)
        load_words(nc.sync, si_raw0[:], 1, 0)
        order_words(co_raw0[:], 0, 0, "co0")

        gain_ps = psum.tile([P, 512], F32, name="bank")
        nc.vector.tensor_copy(
            out=gn_rows[0:2].rearrange("b t (r e) -> b t r e", e=8), in_=gn_raw[:].rearrange("b (r t e) -> b t r e", t=4, e=8)
        )
        for t in range(4):
            nc.tensor.transpose(gain_ps[:, P * t : P * (t + 1)], gn_rows[:, t, :], ident[:])
        gain = gain_ps[:].rearrange("p (t x) -> p x t", t=4)[:, 0:2, :]
        mag = keep.tile([P, 2, 4], F32, name="mag")
        nc.scalar.activation(out=mag[:], in_=gain, func=ACT.Abs)
        mag8 = mag[:].rearrange("p b t -> p (b t)")
        inv_root = keep.tile([P, 8], F32, name="inv_root")
        nc.scalar.activation(out=inv_root[:], in_=mag8, func=ACT.Abs_reciprocal_sqrt, bias=SQRT_FLOOR)
        sign = keep.tile([P, 2, 4], F32, name="sign")
        nc.scalar.activation(out=sign[:], in_=gain, func=ACT.Sign)
        warm = keep.tile([P, 1], F32, name="warm")
        nc.scalar.activation(out=warm[:], in_=inv_root[:, 0:1], func=ACT.Ln)
        root0 = keep.tile([P, 8], F32, name="root0")
        nc.gpsimd.tensor_tensor(out=root0[:], in0=mag8, in1=inv_root[:], op=ALU.mult)
        near_one = keep.tile([P, 8], F32, name="near_one")
        nc.gpsimd.tensor_tensor(out=near_one[:], in0=root0[:], in1=inv_root[:], op=ALU.mult)
        mend = keep.tile([P, 8], F32, name="mend")
        nc.gpsimd.tensor_scalar(out=mend[:], in0=near_one[:], scalar1=-0.5, scalar2=1.5, op0=ALU.mult, op1=ALU.add)
        root = keep.tile([P, 8], F32, name="root")
        nc.gpsimd.tensor_tensor(out=root[:], in0=root0[:], in1=mend[:], op=ALU.mult)

        sc_second = keep.tile([P, 256], I32, name="sc_second", tag="slot_s", align_bytes=64)
        gather_scales(1, 3, sc_second)
        order_scales(0, 1)
        order_scales(1, 1)
        stage_scales(1, 3, sc_second)
        warm_bank = psum.tile([P, 512], F32, name="bank")
        raw_codes = co_raw0[:, 0, :]
        for codes_in, scales in [(raw_codes, planes[1][:, 0:128])] * 2 + [(tab_win[:, 0:256], sc_win[:, 0:128])] * 2:
            nc.tensor.matmul_mx(
                out=warm_bank[:],
                lhsT=raw_codes[:, 0:64].bitcast(U8).bitcast(FP4X4),
                lhsT_scale=scales[:, 0:32].bitcast(U8),
                rhs=codes_in.bitcast(U8).bitcast(FP4X4),
                rhs_scale=scales.bitcast(U8),
                start=True,
                stop=True,
            )
        w_raw1 = [head.tile([P, 2, 256], I32, name="w_raw1_%d" % m, offset=1024 + 2048 * m, align_bytes=64) for m in range(2)]
        for m in range(2):
            load_words(nc.sync, w_raw1[m][:], m, 1)
        move_scales(1)

        got0 = head.tile([P, CHUNK], I32, name="got0", offset=6144, align_bytes=64)
        gather_words(0, got0)
        sc_last = head.tile([P, 128], I32, name="sc_last", offset=6144, align_bytes=64)
        gather_scales(3, 4, sc_last)
        order_words(si_raw0[:], 1, 0, None)
        stage_scales(3, 4, sc_last)

        on_vector = []

        def squares(j0, width, b, order):
            c, o = j0 // CHUNK, j0 % CHUNK
            ts, tlo = TAB_AT[c]
            sq = sq_pool.tile([P, 4, 2, width], F32, name="sq")
            bank = None
            for t, m in order:
                if width == CHUNK or m == 0:
                    bank = psum.tile([P, 512], F32, name="bank")
                lo = 0 if width == CHUNK else m * width
                ws, wlo = W_AT[m][b]
                for a in range(2):
                    nc.tensor.matmul_mx(
                        out=bank[:, lo : lo + width],
                        lhsT=w_codes[m, b][:, 128 * t + 64 * a : 128 * t + 64 * (a + 1)].bitcast(U8).bitcast(FP4X4),
                        lhsT_scale=planes[ws][:, a * WIDTHS[ws] + wlo + 32 * t : a * WIDTHS[ws] + wlo + 32 * (t + 1)].bitcast(U8),
                        rhs=parted[c][:, CHUNK * a + o : CHUNK * a + o + width].bitcast(U8).bitcast(FP4X4),
                        rhs_scale=planes[ts][:, a * WIDTHS[ts] + tlo + o // 4 : a * WIDTHS[ts] + tlo + (o + width) // 4].bitcast(U8),
                        start=(a == 0),
                        stop=(a == 1),
                    )
                scale = root[:, 4 * b + t : 4 * b + t + 1]
                if width == CHUNK and (2 * c + b, t, m) in ON_VECTOR:
                    on_vector.append((bank, scale, sq[:, t, m, :]))
                elif width == CHUNK:
                    nc.scalar.activation(out=sq[:, t, m, :], in_=bank[:], func=ACT.Square, scale=scale)
                elif m == 1:
                    nc.scalar.activation(
                        out=sq[:, t].rearrange("p m w -> p (m w)"), in_=bank[:, 0 : 2 * width], func=ACT.Square, scale=scale
                    )
            return sq

        def add_squares(sq, width, parts, first=False):
            if first:
                h = head.tile([P, width, 4], BF16, name="h0", offset=11264, align_bytes=64)
            else:
                h = h_pool.tile([P, width, 4], BF16, name="h", align_bytes=64)
            step = width // parts
            for u in range(parts):
                cols = slice(step * u, step * (u + 1))
                nc.vector.tensor_tensor(
                    out=h[:, cols, :].rearrange("p (c i) t -> p c t i", i=2),
                    in0=sq[:, :, 0, cols].rearrange("p t (c i) -> p c t i", i=2),
                    in1=sq[:, :, 1, cols].rearrange("p t (c i) -> p c t i", i=2),
                    op=ALU.add,
                )
            return h

        def quantise(h, width, parts):
            codes = hq_pool.tile([P, width], U32, name="codes", align_bytes=64)
            plane = hq_pool.tile([P, width], U8, name="plane", align_bytes=64)
            step = width // parts
            for u in range(parts):
                cols = slice(step * u, step * (u + 1))
                nc.vector.quantize_mx(
                    out=codes[:, cols].bitcast(FP8X4),
                    scales=plane[:, cols],
                    in_=h[:, cols, :].rearrange("p j t -> p (j t)"),
                )
            return codes, plane

        fb_codes = keep.tile([P, 2, N], U32, name="fb_codes", align_bytes=64)
        fb_plane = keep.tile([P, 2, N], U8, name="fb_plane", align_bytes=64)

        def prepare_fb():
            fb_raw = keep.tile([P, 2, 4, N], F32, name="fb_raw", tag="slot_s", align_bytes=64)
            rows = fb.rearrange("(b r t e) n -> b t r e n", b=2, t=4, e=8)
            for b in range(2):
                for t in range(4):
                    nc.sync.dma_start(out=fb_raw[:, b, t, :], in_=rows[b, t])
            fb_bf = [
                head.tile([P, N, 4], BF16, name="fb_bf0", offset=12288, align_bytes=64),
                keep.tile([P, N, 4], BF16, name="fb_bf1", align_bytes=64),
            ]
            for b in range(2):
                (nc.gpsimd, nc.vector)[b].tensor_tensor(
                    out=fb_bf[b][:].rearrange("p (c i) t -> p c t i", i=2),
                    in0=fb_raw[:, b].rearrange("p t (c i) -> p c t i", i=2),
                    in1=sign[:, b, :].unsqueeze(1).unsqueeze(3).to_broadcast([P, N // 2, 4, 2]),
                    op=ALU.mult,
                )
            for b in range(2):
                nc.vector.quantize_mx(
                    out=fb_codes[:, b].bitcast(FP8X4), scales=fb_plane[:, b], in_=fb_bf[b][:].rearrange("p n t -> p (n t)")
                )

        def filters(j0, width, halves):
            for i in range(2):
                bank = psum.tile([P, 512], F32, name="bank")
                lo = 0
                for b in range(2):
                    codes, plane, o = halves[b]
                    nc.tensor.matmul_mx(
                        out=bank[:, lo : lo + width],
                        lhsT=fb_codes[:, b, P * i : P * (i + 1)].bitcast(FP8X4),
                        lhsT_scale=fb_plane[:, b, P * i : P * (i + 1)],
                        rhs=codes[:, o : o + width].bitcast(FP8X4),
                        rhs_scale=plane[:, o : o + width],
                        start=(b == 0),
                        stop=(b == 1),
                    )
                y = y_pool.tile([P, 512], F32, name="y")
                nc.scalar.activation(out=y[:], in_=bank[:], func=ACT.Ln, bias=1.0)
                nc.sync.dma_start(out=out[P * i : P * (i + 1), j0 : j0 + width], in_=y[:])

        def filters_one_bank(j0, width, halves):
            bank = psum.tile([P, 512], F32, name="bank")
            for b in range(2):
                codes, plane, o = halves[b]
                for i in range(2):
                    nc.tensor.matmul_mx(
                        out=bank[:, width * i : width * (i + 1)],
                        lhsT=fb_codes[:, b, P * i : P * (i + 1)].bitcast(FP8X4),
                        lhsT_scale=fb_plane[:, b, P * i : P * (i + 1)],
                        rhs=codes[:, o : o + width].bitcast(FP8X4),
                        rhs_scale=plane[:, o : o + width],
                        start=(b + i == 0),
                        stop=(b + i == 2),
                    )
            y = y_pool.tile([P, 512], F32, name="y")
            nc.scalar.activation(out=y[:, 0 : 2 * width], in_=bank[:, 0 : 2 * width], func=ACT.Ln, bias=1.0)
            nc.sync.dma_start(
                out=out[:, j0 : j0 + width].rearrange("(i p) w -> p i w", p=P),
                in_=y[:, 0 : 2 * width].rearrange("p (i w) -> p i w", i=2),
            )

        def next_words(c):
            if c == 1:
                got = keep.tile([P, CHUNK], I32, name="got1", tag="slot_a", align_bytes=64)
            else:
                got = head.tile([P, CHUNK], I32, name="got%d" % c, offset=(10240, 14336)[c - 2], align_bytes=64)
            gather_words(c, got)

        by_t = [(t, m) for t in range(4) for m in range(2)]
        by_m = [(t, m) for m in range(2) for t in range(4)]
        done = {}
        filtered = []

        def whole(c):
            filters(CHUNK * c, CHUNK, [done[2 * c + b] + (0,) for b in range(2)])
            filtered.append(c)

        waiting = None
        for g in range(2 * CHUNKS - 1):
            c, b = divmod(g, 2)
            sq = squares(CHUNK * c, CHUNK, b, by_m if g == 0 else by_t)
            if g == 0:
                order_words(w_raw1[0][:], 0, 1, "co1")
                order_words(w_raw1[1][:], 1, 1, "si1")
            if g == 0:
                next_words(1)
            if g == 1:
                move_scales(2)
            if on_vector:
                bank, scale, square = on_vector.pop()
                h = add_squares(waiting, CHUNK, 1)
                scaled = x_pool.tile([P, 512], F32, name="scaled")
                nc.vector.tensor_scalar(out=scaled[:], in0=bank[:], scalar1=scale, scalar2=None, op0=ALU.mult)
                done[g - 1] = quantise(h, CHUNK, 1)
                nc.vector.tensor_tensor(out=square, in0=scaled[:], in1=scaled[:], op=ALU.mult)
            elif waiting is not None:
                done[g - 1] = quantise(add_squares(waiting, CHUNK, 2, g == 1), CHUNK, 2)
            if g == 1:
                next_words(2)
                next_words(3)
                prepare_fb()
            if g in FILTERS_AFTER:
                whole(FILTERS_AFTER[g])
            waiting = sq
        j0 = J - CHUNK
        last = [squares(j0 + 256 * u, 256, 1, by_t) for u in range(2)]
        h6 = add_squares(waiting, CHUNK, 1)
        h7 = add_squares(last[0], 256, 1)
        done[6] = quantise(h6, CHUNK, 1)
        pieces = [quantise(h7, 256, 1), quantise(add_squares(last[1], 256, 2), 256, 2)]
        for c in range(CHUNKS - 1):
            if c not in filtered:
                whole(c)
        filters_one_bank(j0, 256, [done[6] + (0,), pieces[0] + (0,)])
        for o in (0, 128):
            filters_one_bank(j0 + 256 + o, 128, [done[6] + (256 + o,), pieces[1] + (o,)])
